import numpy as np
import ml_dtypes


def mxq(x, axis, fmt="e4m3"):
    dtype, down = {"e4m3": (ml_dtypes.float8_e4m3fn, 7), "e5m2": (ml_dtypes.float8_e5m2, 14)}[fmt]
    v = np.moveaxis(np.asarray(x, np.float32).astype(ml_dtypes.bfloat16).astype(np.float64), axis, -1)
    blocks = v.reshape(v.shape[:-1] + (-1, 32))
    amax = np.abs(blocks).max(-1, keepdims=True)
    byte = np.maximum(np.where(amax > 0, np.frexp(amax)[1] - 1 + 127, 0) - down, 1)
    scale = np.exp2(byte - 127.0)
    codes = (blocks / scale).astype(np.float32).astype(dtype).astype(np.float64)
    return np.moveaxis((codes * scale).reshape(v.shape), -1, axis)


WIDE = False


def mx_kscale(k):
    if not WIDE:
        return np.ones(k)
    levels = np.array([10, -10, 5, -5, 0])
    if k % 512:
        return np.exp2(np.random.permutation(np.resize(levels, k // 32))).repeat(32)
    a = np.empty((k // 512, 16))
    for p in range(k // 512):
        a[p, :8] = np.random.permutation(np.resize(levels, 8))
        for g in range(8):
            far = levels[np.abs(levels - a[p, g]) >= 10]
            a[p, g + 8] = far[np.random.randint(len(far))]
    return np.exp2(a.ravel()).repeat(32)


BF16 = ml_dtypes.bfloat16


def bf(x):
    return np.asarray(x, np.float32).astype(BF16)


def f64(x):
    return np.asarray(x).astype(np.float64)


E2M1 = np.array([0.0, 0.5, 1.0, 1.5, 2.0, 3.0, 4.0, 6.0, -0.0, -0.5, -1.0, -1.5, -2.0, -3.0, -4.0, -6.0])


def pack_weight(w, fmt):
    k, n = w.shape
    w = f64(bf(w)).reshape(k // 32, 32, n)
    amax = np.abs(w).max(1)
    if fmt == "e4m3":
        byte = np.frexp(amax)[1] - 1 + 127 - 7
    else:
        mant, ex = np.frexp(amax / 6.0)
        byte = np.where(mant > 0.5, ex, ex - 1) + 127
    byte = np.clip(np.where(amax > 0, byte, 1), 1, 254)
    scaled = (w * np.exp2(127.0 - byte)[:, None, :]).reshape(k, n).astype(np.float32)
    by_word = np.ascontiguousarray(scaled.reshape(k // 512, 128, 4, n).transpose(0, 1, 3, 2))
    if fmt == "e4m3":
        words = by_word.astype(ml_dtypes.float8_e4m3fn).view(np.uint8)
    else:
        c = by_word.astype(ml_dtypes.float4_e2m1fn).view(np.uint8) & 0xF
        words = c[..., 0::2] | (c[..., 1::2] << 4)
    return np.ascontiguousarray(words), np.ascontiguousarray(byte.astype(np.uint8).reshape(k // 512, 16, n))


def unpack_weight(words, scales, fmt):
    g, p, n, _ = words.shape
    if fmt == "e4m3":
        vals = np.ascontiguousarray(words).view(ml_dtypes.float8_e4m3fn).astype(np.float64)
    else:
        nib = np.empty((g, p, n, 4), np.uint8)
        nib[..., 0::2] = words & 0xF
        nib[..., 1::2] = words >> 4
        vals = E2M1[nib]
    vals = vals * np.repeat(np.exp2(scales.astype(np.float64) - 127.0), 8, axis=1)[..., None]
    return vals.transpose(0, 1, 3, 2).reshape(g * 512, n)
def pack4(w):
    words, scales = pack_weight(w, "e2m1")
    return words.reshape(words.shape[0], 128, -1), scales


def unpack4(words, scales):
    return unpack_weight(words.reshape(words.shape[0], 128, -1, 2), scales, "e2m1")


E4M3FN = np.array([(-1.0 if i & 128 else 1.0) * ((1.0 + (i & 7) / 8.0) * 2.0 ** (((i >> 3) & 15) - 7) if i & 120 else (i & 7) * 2.0 ** -9) for i in range(256)])


def e4m3fn_bytes(y):
    return np.clip(np.asarray(y, np.float64), -448.0, 448.0).astype(np.float32).astype(ml_dtypes.float8_e4m3fn).view(np.uint8)


def e4m3fn_values(b):
    return E4M3FN[b]


B, P, K, D, N, G = 2, 256, 3072, 1024, 3072, 128

FP8_MAX = 448.0


def setup_inputs():
    s, t = mx_kscale(K), mx_kscale(D)
    x = np.random.standard_normal((B * P, K)) * s
    w = np.random.standard_normal((K, D)) / np.sqrt(K) / s[:, None]
    x_scale = (np.abs(x).reshape(B * P, K // G, G).max(axis=2) / FP8_MAX).astype(np.float32)
    w_scale = (np.abs(w).reshape(K // G, G, D // G, G).max(axis=(1, 3)) / FP8_MAX).astype(np.float32)
    x_bytes = e4m3fn_bytes(x / np.repeat(f64(x_scale), G, axis=1))
    w_bytes = e4m3fn_bytes(w / np.repeat(np.repeat(f64(w_scale), G, axis=0), G, axis=1))
    v_words, v_scales = pack4(np.random.standard_normal((D, N)) / np.sqrt(D) / t[:, None])
    return {"x_bytes": x_bytes, "x_scale": x_scale,
            "w_bytes": w_bytes, "w_scale": w_scale,
            "gain": bf((1 + 0.1 * np.random.standard_normal(D)) * t),
            "pos": bf(0.5 * np.random.standard_normal((P, D)) * t),
            "v_words": v_words, "v_scales": v_scales,
            "bias": bf(0.3 * np.random.standard_normal(N))}


def reference(x_bytes, x_scale, w_bytes, w_scale, gain, pos, v_words, v_scales, bias):
    x = e4m3fn_values(x_bytes) * np.repeat(f64(x_scale), G, axis=1)
    w = e4m3fn_values(w_bytes) * np.repeat(np.repeat(f64(w_scale), G, axis=0), G, axis=1)
    e = mxq(x, 1, "e4m3") @ mxq(w, 0, "e4m3")
    h = (e * f64(gain)).reshape(B, P, D) + f64(pos)
    h = h.reshape(B * P, D)
    y = mxq(h, 1, "e4m3") @ unpack4(v_words, v_scales)
    return y + f64(bias)

@@ -1,0 +1,253 @@
+from contextlib import ExitStack
+
+import concourse.mybir as mybir
+from concourse.masks import make_identity
+
+F32 = mybir.dt.float32
+BF16 = mybir.dt.bfloat16
+I32 = mybir.dt.int32
+U32 = mybir.dt.uint32
+U8 = mybir.dt.uint8
+FP8 = mybir.dt.float8_e4m3fn
+FP8X4 = mybir.dt.float8_e4m3fn_x4
+FP4X4 = mybir.dt.float4_e2m1fn_x4
+MULT = mybir.AluOpType.mult
+ADD = mybir.AluOpType.add
+COPY = mybir.ActivationFunctionType.Copy
+
+P = 128
+TOK, K, D, N = 512, 3072, 1024, 3072
+G1 = K // 512
+FLOPS = 2 * TOK * K * D + 2 * TOK * D * N
+
+
+def tile_patch_embed_qkv_d4_kernel(tc, x_bytes, x_scale, w_bytes, w_scale, gain, pos, v_words, v_scales, bias, out):
+    nc = tc.nc
+    with ExitStack() as ctx:
+        keep = ctx.enter_context(tc.tile_pool(name="keep", bufs=1))
+        stage = ctx.enter_context(tc.tile_pool(name="stage", bufs=3))
+        psum = ctx.enter_context(tc.psum_pool(name="psum", bufs=1))
+        ctx.enter_context(tc.manual_schedule())
+
+        def bank(b):
+            return psum.tile([P, 512], F32, name="bank%d" % b)
+
+        xs = keep.tile([P, 4 * 24], F32, name="xs")
+        nc.sync.dma_start(out=xs[:].rearrange("p (i c) -> p i c", i=4), in_=x_scale.rearrange("(i p) c -> p i c", p=P))
+        wall = keep.tile([P, 192], F32, name="wall")
+        nc.scalar.dma_start(out=wall[:], in_=w_scale.rearrange("c d -> (c d)").partition_broadcast(P))
+
+        x_rows = x_bytes.rearrange("(i p) k -> p i k", p=P)
+        xb, wb = {}, {}
+
+        def load_x(g):
+            xb[g] = keep.tile([P, 2048], U8, name="xb%d" % g)
+            nc.sync.dma_start(out=xb[g][:].rearrange("p (i k) -> p i k", i=4), in_=x_rows[:, :, 512 * g:512 * g + 512])
+
+        def load_w(g, hf):
+            wb[g, hf] = keep.tile([P, 2048], U8, name="wb%d_%d" % (g, hf))
+            nc.sync.dma_start(
+                out=wb[g, hf][:].rearrange("p (t n) -> p t n", t=4),
+                in_=w_bytes[512 * g:512 * g + 512, 512 * hf:512 * hf + 512].rearrange("(p t) n -> p t n", t=4))
+
+        for g in range(G1):
+            load_x(g)
+            load_w(g, 0)
+        pos_sb = keep.tile([P, 2048], BF16, name="pos_sb")
+        nc.sync.dma_start(out=pos_sb[:].rearrange("p (i j) -> p i j", i=2), in_=pos.rearrange("(i p) j -> p i j", p=P))
+        gain_b = keep.tile([P, 8], BF16, name="gain_b")
+        nc.sync.dma_start(out=gain_b[:].rearrange("p (h t) -> p h t", h=2), in_=gain.rearrange("(h p t) -> p h t", h=2, t=4))
+        for g in range(G1):
+            load_w(g, 1)
+        vw = [keep.tile([P, 6144], U8, name="vw%d" % h, align_bytes=64) for h in range(2)]
+        for h in range(2):
+            nc.sync.dma_start(out=vw[h][:].bitcast(I32), in_=v_words[h].bitcast(I32))
+        vs = keep.tile([P, 2 * N], U8, name="vs", align_bytes=64)
+        nc.gpsimd.memset(vs[:].bitcast(I32), 0)
+        for q in range(4):
+            nc.sync.dma_start(
+                out=vs[32 * q:32 * q + 4, :].rearrange("p (h n) -> p h n", h=2).bitcast(I32),
+                in_=v_scales[:, 4 * q:4 * q + 4, :].rearrange("h r n -> r h n").bitcast(I32))
+        bias_sb = keep.tile([P, N], BF16, name="bias_sb")
+        nc.sync.dma_start(out=bias_sb[:], in_=bias.partition_broadcast(P))
+
+        ident = keep.tile([P, P], F32, name="ident")
+        make_identity(nc, ident[:])
+        wsc = keep.tile([P, G1 * 8], F32, name="wsc")
+        for q in range(4):
+            rows = slice(32 * q, 32 * q + 32)
+            nc.gpsimd.tensor_copy(
+                out=wsc[rows, :].rearrange("p (g d) -> p g d", g=G1),
+                in_=wall[rows, :].rearrange("p (g q d) -> p q g d", q=4, d=8)[:, q])
+        gain_f = keep.tile([P, 8], F32, name="gain_f")
+        nc.gpsimd.tensor_copy(out=gain_f[:], in_=gain_b[:])
+
+        xw, xint, xq, xqs = {}, {}, {}, {}
+        xbank = {}
+
+        def x_widen(g):
+            xw[g] = stage.tile([P, 2048], BF16, name="xw")
+            for i in range(4):
+                for c in range(4):
+                    cols = slice(512 * i + 128 * c, 512 * i + 128 * c + 128)
+                    col = 24 * i + 4 * g + c
+                    nc.vector.tensor_scalar(out=xw[g][:, cols], in0=xb[g][:, cols].bitcast(FP8), scalar1=xs[:, col:col + 1], scalar2=None, op0=MULT)
+
+        def x_turn(g):
+            words = xw[g][:].bitcast(F32)
+            for h in range(2):
+                xbank[g, h] = bank(4 + (2 * g + h) % 4)
+                for i in range(2):
+                    for u in range(2):
+                        first = 256 * (2 * h + i)
+                        at = 128 * (2 * i + u)
+                        nc.tensor.transpose(xbank[g, h][:, at:at + 128], words[:, first + u:first + 256:2], ident[:])
+
+        def x_out(g):
+            xint[g] = stage.tile([P, 2048], BF16, name="xint", align_bytes=64)
+            for h in range(2):
+                nc.scalar.copy(
+                    out=xint[g][:, 1024 * h:1024 * h + 1024].bitcast(F32).rearrange("p (i r u) -> p i r u", i=2, u=2),
+                    in_=xbank[g, h][:].rearrange("p (i u r) -> p i r u", i=2, u=2))
+
+        def x_quant(g):
+            xq[g] = keep.tile([P, 512], U32, name="xq%d" % g, align_bytes=64)
+            xqs[g] = keep.tile([P, 512], U8, name="xqs%d" % g, align_bytes=64)
+            nc.vector.quantize_mx(out=xq[g][:].bitcast(FP8X4), scales=xqs[g][:], in_=xint[g][:])
+
+        ww, wint, wq, wqs = {}, {}, {}, {}
+
+        def w_widen(g, hf, part):
+            if part == 0:
+                ww[g, hf] = keep.tile([P, 2048], BF16, name="ww%d" % ((g + 6 * hf) % 8))
+            cols = slice(1024 * part, 1024 * part + 1024)
+            nc.scalar.copy(out=ww[g, hf][:, cols], in_=wb[g, hf][:, cols].bitcast(FP8))
+
+        def w_scale_in(g, hf):
+            wint[g, hf] = stage.tile([P, 2048], BF16, name="wint", align_bytes=64)
+            src = ww[g, hf][:].rearrange("p (j b m t) -> p b t m j", j=4, b=4, t=4)
+            dst = wint[g, hf][:].rearrange("p (t b m j) -> p b t m j", t=4, b=4, j=4)
+            for b in range(4):
+                col = 8 * g + 4 * hf + b
+                nc.vector.tensor_scalar(out=dst[:, b], in0=src[:, b], scalar1=wsc[:, col:col + 1], scalar2=None, op0=MULT)
+
+        def w_quant(g, hf):
+            wq[g, hf] = stage.tile([P, 512], U32, name="wq", align_bytes=64)
+            wqs[g, hf] = stage.tile([P, 512], U8, name="wqs", align_bytes=64)
+            nc.vector.quantize_mx(out=wq[g, hf][:].bitcast(FP8X4), scales=wqs[g, hf][:], in_=wint[g, hf][:])
+
+        e = {}
+
+        def mm1(g, hf):
+            for t in range(4):
+                if g == 0:
+                    e[hf, t] = bank(4 * hf + t)
+                nc.tensor.matmul_mx(
+                    out=e[hf, t][:],
+                    lhsT=wq[g, hf][:, 128 * t:128 * t + 128].bitcast(FP8X4), lhsT_scale=wqs[g, hf][:, 128 * t:128 * t + 128],
+                    rhs=xq[g][:].bitcast(FP8X4), rhs_scale=xqs[g][:], start=(g == 0), stop=(g == G1 - 1))
+
+        pos_t = keep.tile([P, 2048], BF16, name="pos_t")
+
+        def pos_turn():
+            words = pos_sb[:].bitcast(F32)
+            for hf in range(2):
+                pb = bank(4 + hf)
+                for i in range(2):
+                    for u in range(2):
+                        first = 512 * i + 256 * hf
+                        at = 128 * (2 * i + u)
+                        nc.tensor.transpose(pb[:, at:at + 128], words[:, first + u:first + 256:2], ident[:])
+                nc.scalar.copy(
+                    out=pos_t[:, 1024 * hf:1024 * hf + 1024].bitcast(F32).rearrange("p (i r u) -> p i r u", i=2, u=2),
+                    in_=pb[:].rearrange("p (i u r) -> p i r u", i=2, u=2))
+
+        hs, hint = {}, {}
+        hq = [keep.tile([P, 512], U32, name="hq%d" % h, align_bytes=64) for h in range(2)]
+        hqs = [keep.tile([P, 512], U8, name="hqs%d" % h, align_bytes=64) for h in range(2)]
+
+        def h_gain(hf, t):
+            if t == 0:
+                hs[hf] = keep.tile([P, 2048], F32, name="hs%d" % hf)
+                hint[hf] = keep.tile([P, 2048], BF16, name="hint%d" % hf, align_bytes=64)
+            nc.scalar.activation(out=hs[hf][:, 512 * t:512 * t + 512], in_=e[hf, t][:], func=COPY, scale=gain_f[:, 4 * hf + t:4 * hf + t + 1])
+
+        def h_pos(hf, a):
+            nc.vector.tensor_tensor(
+                out=hint[hf][:, 1024 * a:1024 * a + 1024].rearrange("p (r t) -> p r t", t=4),
+                in0=hs[hf][:].rearrange("p (t a r) -> p a r t", t=4, a=2)[:, a],
+                in1=pos_t[:, 1024 * hf:1024 * hf + 1024].rearrange("p (r t) -> p r t", t=4), op=ADD)
+
+        def h_quant(hf, a):
+            nc.vector.quantize_mx(out=hq[hf][:, 256 * a:256 * a + 256].bitcast(FP8X4), scales=hqs[hf][:, 256 * a:256 * a + 256], in_=hint[hf][:, 1024 * a:1024 * a + 1024])
+
+        ob, ot = {}, {}
+
+        def mm2(n, h):
+            i, c = divmod(n, 6)
+            if h == 0:
+                ob[n] = bank(n % 8)
+            nc.tensor.matmul_mx(
+                out=ob[n][:],
+                lhsT=hq[h][:, 128 * i:128 * i + 128].bitcast(FP8X4), lhsT_scale=hqs[h][:, 128 * i:128 * i + 128],
+                rhs=vw[h][:, 1024 * c:1024 * c + 1024].bitcast(FP4X4), rhs_scale=vs[:, N * h + 512 * c:N * h + 512 * c + 512],
+                start=(h == 0), stop=(h == 1))
+
+        def finish(n):
+            i, c = divmod(n, 6)
+            ot[n] = stage.tile([P, 512], F32, name="ot%d" % (n % 2))
+            nc.vector.tensor_tensor(out=ot[n][:], in0=ob[n][:], in1=bias_sb[:, 512 * c:512 * c + 512], op=ADD)
+            nc.sync.dma_start(out=out[128 * i:128 * i + 128, 512 * c:512 * c + 512], in_=ot[n][:])
+
+        w_widen(0, 0, 0)
+        x_widen(0)
+        x_turn(0)
+        w_widen(0, 0, 1)
+        x_out(0)
+        extra = [(g, 1, part) for g in range(G1) for part in range(2)]
+        for g in range(G1):
+            w_scale_in(g, 0)
+            if g + 1 < G1:
+                x_widen(g + 1)
+                x_turn(g + 1)
+                w_widen(g + 1, 0, 0)
+            x_quant(g)
+            w_quant(g, 0)
+            if g + 1 < G1:
+                x_out(g + 1)
+                w_widen(g + 1, 0, 1)
+                if g >= 1 and extra:
+                    w_widen(*extra.pop(0))
+            mm1(g, 0)
+        pos_turn()
+        w_widen(*extra.pop(0))
+        w_widen(*extra.pop(0))
+        w_scale_in(0, 1)
+        for g in range(G1):
+            if g + 1 < G1:
+                w_scale_in(g + 1, 1)
+            w_quant(g, 1)
+            mm1(g, 1)
+            if g < 4:
+                h_gain(0, g)
+            if g == 4:
+                h_pos(0, 0)
+                h_pos(0, 1)
+            for j in range(2):
+                if extra:
+                    w_widen(*extra.pop(0))
+        h_quant(0, 0)
+        h_quant(0, 1)
+        for n in range(4):
+            mm2(n, 0)
+        for t in range(4):
+            h_gain(1, t)
+        h_pos(1, 0)
+        h_pos(1, 1)
+        h_quant(1, 0)
+        h_quant(1, 1)
+        for n in range(24):
+            if n >= 4:
+                mm2(n, 0)
+            mm2(n, 1)
+            finish(n)

@@ -18,6 +18,9 @@ COPY = mybir.ActivationFunctionType.Copy
 P = 128
 TOK, K, D, N = 512, 3072, 1024, 3072
 G1 = K // 512
+X_ON_SCALAR = ()
+MORE = (1, 1, 1, 1, 2, 2)
+ON_GPSIMD = ()
 FLOPS = 2 * TOK * K * D + 2 * TOK * D * N
 
 
@@ -26,6 +29,7 @@ def tile_patch_embed_qkv_d4_kernel(tc, x_bytes, x_scale, w_bytes, w_scale, gain,
     with ExitStack() as ctx:
         keep = ctx.enter_context(tc.tile_pool(name="keep", bufs=1))
         stage = ctx.enter_context(tc.tile_pool(name="stage", bufs=3))
+        outs = ctx.enter_context(tc.tile_pool(name="outs", bufs=5))
         psum = ctx.enter_context(tc.psum_pool(name="psum", bufs=1))
         ctx.enter_context(tc.manual_schedule())
 
@@ -85,30 +89,33 @@ def tile_patch_embed_qkv_d4_kernel(tc, x_bytes, x_scale, w_bytes, w_scale, gain,
         xw, xint, xq, xqs = {}, {}, {}, {}
         xbank = {}
 
-        def x_widen(g):
-            xw[g] = stage.tile([P, 2048], BF16, name="xw")
-            for i in range(4):
+        def x_widen(g, tiles):
+            if g not in xw:
+                xw[g] = stage.tile([P, 2048], BF16, name="xw")
+            for i in tiles:
                 for c in range(4):
                     cols = slice(512 * i + 128 * c, 512 * i + 128 * c + 128)
                     col = 24 * i + 4 * g + c
-                    nc.vector.tensor_scalar(out=xw[g][:, cols], in0=xb[g][:, cols].bitcast(FP8), scalar1=xs[:, col:col + 1], scalar2=None, op0=MULT)
+                    if i in X_ON_SCALAR:
+                        nc.scalar.activation(out=xw[g][:, cols], in_=xb[g][:, cols].bitcast(FP8), func=COPY, scale=xs[:, col:col + 1])
+                    else:
+                        nc.vector.tensor_scalar(out=xw[g][:, cols], in0=xb[g][:, cols].bitcast(FP8), scalar1=xs[:, col:col + 1], scalar2=None, op0=MULT)
 
-        def x_turn(g):
+        def x_turn(g, h):
             words = xw[g][:].bitcast(F32)
-            for h in range(2):
-                xbank[g, h] = bank(4 + (2 * g + h) % 4)
-                for i in range(2):
-                    for u in range(2):
-                        first = 256 * (2 * h + i)
-                        at = 128 * (2 * i + u)
-                        nc.tensor.transpose(xbank[g, h][:, at:at + 128], words[:, first + u:first + 256:2], ident[:])
+            xbank[g, h] = bank(4 + (2 * g + h) % 4)
+            for i in range(2):
+                for u in range(2):
+                    first = 256 * (2 * h + i)
+                    at = 128 * (2 * i + u)
+                    nc.tensor.transpose(xbank[g, h][:, at:at + 128], words[:, first + u:first + 256:2], ident[:])
 
-        def x_out(g):
-            xint[g] = stage.tile([P, 2048], BF16, name="xint", align_bytes=64)
-            for h in range(2):
-                nc.scalar.copy(
-                    out=xint[g][:, 1024 * h:1024 * h + 1024].bitcast(F32).rearrange("p (i r u) -> p i r u", i=2, u=2),
-                    in_=xbank[g, h][:].rearrange("p (i u r) -> p i r u", i=2, u=2))
+        def x_out(g, h):
+            if h == 0:
+                xint[g] = stage.tile([P, 2048], BF16, name="xint", align_bytes=64)
+            nc.scalar.copy(
+                out=xint[g][:, 1024 * h:1024 * h + 1024].bitcast(F32).rearrange("p (i r u) -> p i r u", i=2, u=2),
+                in_=xbank[g, h][:].rearrange("p (i u r) -> p i r u", i=2, u=2))
 
         def x_quant(g):
             xq[g] = keep.tile([P, 512], U32, name="xq%d" % g, align_bytes=64)
@@ -119,14 +126,14 @@ def tile_patch_embed_qkv_d4_kernel(tc, x_bytes, x_scale, w_bytes, w_scale, gain,
 
         def w_widen(g, hf, part):
             if part == 0:
-                ww[g, hf] = keep.tile([P, 2048], BF16, name="ww%d" % ((g + 6 * hf) % 8))
+                ww[g, hf] = keep.tile([P, 2048], BF16, name="ww%d" % ((g + 6 * hf) % 7))
             cols = slice(1024 * part, 1024 * part + 1024)
             nc.scalar.copy(out=ww[g, hf][:, cols], in_=wb[g, hf][:, cols].bitcast(FP8))
 
         def w_scale_in(g, hf):
             wint[g, hf] = stage.tile([P, 2048], BF16, name="wint", align_bytes=64)
-            src = ww[g, hf][:].rearrange("p (j b m t) -> p b t m j", j=4, b=4, t=4)
-            dst = wint[g, hf][:].rearrange("p (t b m j) -> p b t m j", t=4, b=4, j=4)
+            src = ww[g, hf][:].rearrange("p (j b m t) -> p b m t j", j=4, b=4, t=4)
+            dst = wint[g, hf][:].rearrange("p (t b m j) -> p b m t j", t=4, b=4, j=4)
             for b in range(4):
                 col = 8 * g + 4 * hf + b
                 nc.vector.tensor_scalar(out=dst[:, b], in0=src[:, b], scalar1=wsc[:, col:col + 1], scalar2=None, op0=MULT)
@@ -166,20 +173,24 @@ def tile_patch_embed_qkv_d4_kernel(tc, x_bytes, x_scale, w_bytes, w_scale, gain,
         hq = [keep.tile([P, 512], U32, name="hq%d" % h, align_bytes=64) for h in range(2)]
         hqs = [keep.tile([P, 512], U8, name="hqs%d" % h, align_bytes=64) for h in range(2)]
 
-        def h_gain(hf, t):
-            if t == 0:
-                hs[hf] = keep.tile([P, 2048], F32, name="hs%d" % hf)
+        def h_gain(hf, t, a):
+            if (hf, 0) not in hs:
+                hs[hf, 0] = keep.tile([P, 2048], F32, name="hs%d" % hf)
                 hint[hf] = keep.tile([P, 2048], BF16, name="hint%d" % hf, align_bytes=64)
-            nc.scalar.activation(out=hs[hf][:, 512 * t:512 * t + 512], in_=e[hf, t][:], func=COPY, scale=gain_f[:, 4 * hf + t:4 * hf + t + 1])
+            at = 1024 * a + 256 * t
+            nc.scalar.activation(out=hs[hf, 0][:, at:at + 256], in_=e[hf, t][:, 256 * a:256 * a + 256], func=COPY, scale=gain_f[:, 4 * hf + t:4 * hf + t + 1])
 
-        def h_pos(hf, a):
+        def h_pos(hf, i):
+            a, r = divmod(i, 2)
+            rows = slice(128 * r, 128 * r + 128)
             nc.vector.tensor_tensor(
-                out=hint[hf][:, 1024 * a:1024 * a + 1024].rearrange("p (r t) -> p r t", t=4),
-                in0=hs[hf][:].rearrange("p (t a r) -> p a r t", t=4, a=2)[:, a],
-                in1=pos_t[:, 1024 * hf:1024 * hf + 1024].rearrange("p (r t) -> p r t", t=4), op=ADD)
+                out=hint[hf][:, 512 * i:512 * i + 512].rearrange("p (r t) -> p r t", t=4),
+                in0=hs[hf, 0][:, 1024 * a:1024 * a + 1024].rearrange("p (t r) -> p r t", t=4)[:, rows],
+                in1=pos_t[:, 1024 * hf:1024 * hf + 1024].rearrange("p (r t) -> p r t", t=4)[:, rows], op=ADD)
 
-        def h_quant(hf, a):
-            nc.vector.quantize_mx(out=hq[hf][:, 256 * a:256 * a + 256].bitcast(FP8X4), scales=hqs[hf][:, 256 * a:256 * a + 256], in_=hint[hf][:, 1024 * a:1024 * a + 1024])
+        def h_quant(hf, i, n=1):
+            w = slice(128 * i, 128 * (i + n))
+            nc.vector.quantize_mx(out=hq[hf][:, w].bitcast(FP8X4), scales=hqs[hf][:, w], in_=hint[hf][:, 512 * i:512 * (i + n)])
 
         ob, ot = {}, {}
 
@@ -195,33 +206,61 @@ def tile_patch_embed_qkv_d4_kernel(tc, x_bytes, x_scale, w_bytes, w_scale, gain,
 
         def finish(n):
             i, c = divmod(n, 6)
-            ot[n] = stage.tile([P, 512], F32, name="ot%d" % (n % 2))
-            nc.vector.tensor_tensor(out=ot[n][:], in0=ob[n][:], in1=bias_sb[:, 512 * c:512 * c + 512], op=ADD)
-            nc.sync.dma_start(out=out[128 * i:128 * i + 128, 512 * c:512 * c + 512], in_=ot[n][:])
+            if c % 2 == 0:
+                ot[n // 2] = outs.tile([P, 1024], F32, name="ot")
+            o = ot[n // 2][:, 512 * (c % 2):512 * (c % 2) + 512]
+            b = bias_sb[:, 512 * c:512 * c + 512]
+            if n in ON_GPSIMD:
+                raw = stage.tile([P, 512], F32, name="raw")
+                nc.scalar.copy(out=raw[:], in_=ob[n][:])
+                nc.gpsimd.tensor_tensor(out=o, in0=raw[:], in1=b, op=ADD)
+            else:
+                nc.vector.tensor_tensor(out=o, in0=ob[n][:], in1=b, op=ADD)
+            if n >= 22:
+                nc.sync.dma_start(out=out[128 * i:128 * i + 128, 512 * c:512 * c + 512], in_=o)
+            elif c % 2 == 1:
+                nc.sync.dma_start(out=out[128 * i:128 * i + 128, 512 * c - 512:512 * c + 512], in_=ot[n // 2][:])
 
-        w_widen(0, 0, 0)
-        x_widen(0)
-        x_turn(0)
-        w_widen(0, 0, 1)
-        x_out(0)
+        on_vector = [i for i in range(4) if i not in X_ON_SCALAR]
+        on_scalar = list(X_ON_SCALAR)
         extra = [(g, 1, part) for g in range(G1) for part in range(2)]
+
+        def more(k):
+            for j in range(k):
+                if extra:
+                    w_widen(*extra.pop(0))
+
+        def w_wide(g):
+            if g < G1:
+                w_widen(g, 0, 0)
+                w_widen(g, 0, 1)
+
+        x_widen(0, on_scalar)
+        x_widen(0, on_vector)
+        w_wide(0)
+        for h in range(2):
+            x_turn(0, h)
+            x_out(0, h)
+        x_widen(1, on_scalar)
+        w_wide(1)
         for g in range(G1):
             w_scale_in(g, 0)
             if g + 1 < G1:
-                x_widen(g + 1)
-                x_turn(g + 1)
-                w_widen(g + 1, 0, 0)
+                x_widen(g + 1, on_vector)
+                x_turn(g + 1, 0)
+                x_turn(g + 1, 1)
             x_quant(g)
             w_quant(g, 0)
+            if g + 2 < G1:
+                x_widen(g + 2, on_scalar)
+            w_wide(g + 2)
             if g + 1 < G1:
-                x_out(g + 1)
-                w_widen(g + 1, 0, 1)
-                if g >= 1 and extra:
-                    w_widen(*extra.pop(0))
+                x_out(g + 1, 0)
+                x_out(g + 1, 1)
+            else:
+                pos_turn()
+            more(MORE[g])
             mm1(g, 0)
-        pos_turn()
-        w_widen(*extra.pop(0))
-        w_widen(*extra.pop(0))
         w_scale_in(0, 1)
         for g in range(G1):
             if g + 1 < G1:
@@ -229,19 +268,21 @@ def tile_patch_embed_qkv_d4_kernel(tc, x_bytes, x_scale, w_bytes, w_scale, gain,
             w_quant(g, 1)
             mm1(g, 1)
             if g < 4:
-                h_gain(0, g)
+                h_gain(0, g, 0)
+                h_gain(0, g, 1)
             if g == 4:
                 h_pos(0, 0)
                 h_pos(0, 1)
-            for j in range(2):
-                if extra:
-                    w_widen(*extra.pop(0))
-        h_quant(0, 0)
-        h_quant(0, 1)
+            more(2)
+        h_pos(0, 2)
+        h_quant(0, 0, 2)
+        h_pos(0, 3)
+        h_quant(0, 2, 2)
         for n in range(4):
             mm2(n, 0)
-        for t in range(4):
-            h_gain(1, t)
+        for a in range(2):
+            for t in range(4):
+                h_gain(1, t, a)
         h_pos(1, 0)
         h_pos(1, 1)
         h_quant(1, 0)
@@ -250,4 +291,10 @@ def tile_patch_embed_qkv_d4_kernel(tc, x_bytes, x_scale, w_bytes, w_scale, gain,
             if n >= 4:
                 mm2(n, 0)
             mm2(n, 1)
+            if n == 0:
+                h_pos(1, 2)
+            if n == 1:
+                h_pos(1, 3)
+            if n == 2:
+                h_quant(1, 2, 2)
             finish(n)

@@ -18,9 +18,10 @@ COPY = mybir.ActivationFunctionType.Copy
 P = 128
 TOK, K, D, N = 512, 3072, 1024, 3072
 G1 = K // 512
-X_ON_SCALAR = ()
-MORE = (1, 1, 1, 1, 2, 2)
-ON_GPSIMD = ()
+XS = ((), (), (), (), (), ())
+V_SCALES = tuple(range(12))
+AHEAD = 4
+ON_GPSIMD = (3, 7, 11, 15, 19)
 FLOPS = 2 * TOK * K * D + 2 * TOK * D * N
 
 
@@ -29,6 +30,7 @@ def tile_patch_embed_qkv_d4_kernel(tc, x_bytes, x_scale, w_bytes, w_scale, gain,
     with ExitStack() as ctx:
         keep = ctx.enter_context(tc.tile_pool(name="keep", bufs=1))
         stage = ctx.enter_context(tc.tile_pool(name="stage", bufs=3))
+        wide = ctx.enter_context(tc.tile_pool(name="wide", bufs=AHEAD + 2))
         outs = ctx.enter_context(tc.tile_pool(name="outs", bufs=5))
         psum = ctx.enter_context(tc.psum_pool(name="psum", bufs=1))
         ctx.enter_context(tc.manual_schedule())
@@ -96,7 +98,7 @@ def tile_patch_embed_qkv_d4_kernel(tc, x_bytes, x_scale, w_bytes, w_scale, gain,
                 for c in range(4):
                     cols = slice(512 * i + 128 * c, 512 * i + 128 * c + 128)
                     col = 24 * i + 4 * g + c
-                    if i in X_ON_SCALAR:
+                    if i in XS[g]:
                         nc.scalar.activation(out=xw[g][:, cols], in_=xb[g][:, cols].bitcast(FP8), func=COPY, scale=xs[:, col:col + 1])
                     else:
                         nc.vector.tensor_scalar(out=xw[g][:, cols], in0=xb[g][:, cols].bitcast(FP8), scalar1=xs[:, col:col + 1], scalar2=None, op0=MULT)
@@ -124,69 +126,73 @@ def tile_patch_embed_qkv_d4_kernel(tc, x_bytes, x_scale, w_bytes, w_scale, gain,
 
         ww, wint, wq, wqs = {}, {}, {}, {}
 
-        def w_widen(g, hf, part):
-            if part == 0:
-                ww[g, hf] = keep.tile([P, 2048], BF16, name="ww%d" % ((g + 6 * hf) % 7))
-            cols = slice(1024 * part, 1024 * part + 1024)
-            nc.scalar.copy(out=ww[g, hf][:, cols], in_=wb[g, hf][:, cols].bitcast(FP8))
+        def w_widen(u):
+            g, hf = u % G1, u // G1
+            ww[u] = wide.tile([P, 2048], BF16, name="ww")
+            if u in V_SCALES:
+                nc.scalar.copy(out=ww[u][:], in_=wb[g, hf][:].bitcast(FP8))
+            else:
+                nc.vector.tensor_copy(out=ww[u][:], in_=wb[g, hf][:].bitcast(FP8))
 
-        def w_scale_in(g, hf):
-            wint[g, hf] = stage.tile([P, 2048], BF16, name="wint", align_bytes=64)
-            src = ww[g, hf][:].rearrange("p (j b m t) -> p b m t j", j=4, b=4, t=4)
-            dst = wint[g, hf][:].rearrange("p (t b m j) -> p b m t j", t=4, b=4, j=4)
+        def w_scale_in(u):
+            g, hf = u % G1, u // G1
+            wint[u] = stage.tile([P, 2048], BF16, name="wint", align_bytes=64)
+            src = ww[u][:].rearrange("p (j b m t) -> p b m t j", j=4, b=4, t=4)
+            dst = wint[u][:].rearrange("p (t b m j) -> p b m t j", t=4, b=4, j=4)
             for b in range(4):
                 col = 8 * g + 4 * hf + b
-                nc.vector.tensor_scalar(out=dst[:, b], in0=src[:, b], scalar1=wsc[:, col:col + 1], scalar2=None, op0=MULT)
+                if u in V_SCALES:
+                    nc.vector.tensor_scalar(out=dst[:, b], in0=src[:, b], scalar1=wsc[:, col:col + 1], scalar2=None, op0=MULT)
+                else:
+                    nc.scalar.activation(out=dst[:, b], in_=src[:, b], func=COPY, scale=wsc[:, col:col + 1])
 
-        def w_quant(g, hf):
-            wq[g, hf] = stage.tile([P, 512], U32, name="wq", align_bytes=64)
-            wqs[g, hf] = stage.tile([P, 512], U8, name="wqs", align_bytes=64)
-            nc.vector.quantize_mx(out=wq[g, hf][:].bitcast(FP8X4), scales=wqs[g, hf][:], in_=wint[g, hf][:])
+        def w_quant(u):
+            wq[u] = stage.tile([P, 512], U32, name="wq", align_bytes=64)
+            wqs[u] = stage.tile([P, 512], U8, name="wqs", align_bytes=64)
+            nc.vector.quantize_mx(out=wq[u][:].bitcast(FP8X4), scales=wqs[u][:], in_=wint[u][:])
 
         e = {}
 
-        def mm1(g, hf):
+        def mm1(u):
+            g, hf = u % G1, u // G1
             for t in range(4):
                 if g == 0:
                     e[hf, t] = bank(4 * hf + t)
                 nc.tensor.matmul_mx(
                     out=e[hf, t][:],
-                    lhsT=wq[g, hf][:, 128 * t:128 * t + 128].bitcast(FP8X4), lhsT_scale=wqs[g, hf][:, 128 * t:128 * t + 128],
+                    lhsT=wq[u][:, 128 * t:128 * t + 128].bitcast(FP8X4), lhsT_scale=wqs[u][:, 128 * t:128 * t + 128],
                     rhs=xq[g][:].bitcast(FP8X4), rhs_scale=xqs[g][:], start=(g == 0), stop=(g == G1 - 1))
 
         pos_t = keep.tile([P, 2048], BF16, name="pos_t")
 
-        def pos_turn():
+        def pos_turn(hf):
             words = pos_sb[:].bitcast(F32)
-            for hf in range(2):
-                pb = bank(4 + hf)
-                for i in range(2):
-                    for u in range(2):
-                        first = 512 * i + 256 * hf
-                        at = 128 * (2 * i + u)
-                        nc.tensor.transpose(pb[:, at:at + 128], words[:, first + u:first + 256:2], ident[:])
-                nc.scalar.copy(
-                    out=pos_t[:, 1024 * hf:1024 * hf + 1024].bitcast(F32).rearrange("p (i r u) -> p i r u", i=2, u=2),
-                    in_=pb[:].rearrange("p (i u r) -> p i r u", i=2, u=2))
+            pb = bank(6 + hf)
+            for i in range(2):
+                for u in range(2):
+                    first = 512 * i + 256 * hf
+                    at = 128 * (2 * i + u)
+                    nc.tensor.transpose(pb[:, at:at + 128], words[:, first + u:first + 256:2], ident[:])
+            nc.scalar.copy(
+                out=pos_t[:, 1024 * hf:1024 * hf + 1024].bitcast(F32).rearrange("p (i r u) -> p i r u", i=2, u=2),
+                in_=pb[:].rearrange("p (i u r) -> p i r u", i=2, u=2))
 
         hs, hint = {}, {}
         hq = [keep.tile([P, 512], U32, name="hq%d" % h, align_bytes=64) for h in range(2)]
         hqs = [keep.tile([P, 512], U8, name="hqs%d" % h, align_bytes=64) for h in range(2)]
 
-        def h_gain(hf, t, a):
-            if (hf, 0) not in hs:
-                hs[hf, 0] = keep.tile([P, 2048], F32, name="hs%d" % hf)
+        def h_gain(hf, t, lo, hi):
+            if hf not in hs:
+                hs[hf] = keep.tile([P, 2048], F32, name="hs%d" % hf)
                 hint[hf] = keep.tile([P, 2048], BF16, name="hint%d" % hf, align_bytes=64)
-            at = 1024 * a + 256 * t
-            nc.scalar.activation(out=hs[hf, 0][:, at:at + 256], in_=e[hf, t][:, 256 * a:256 * a + 256], func=COPY, scale=gain_f[:, 4 * hf + t:4 * hf + t + 1])
+            nc.scalar.activation(out=hs[hf][:, 512 * t + lo:512 * t + hi], in_=e[hf, t][:, lo:hi], func=COPY, scale=gain_f[:, 4 * hf + t:4 * hf + t + 1])
 
         def h_pos(hf, i):
-            a, r = divmod(i, 2)
-            rows = slice(128 * r, 128 * r + 128)
+            r = i % 2
             nc.vector.tensor_tensor(
                 out=hint[hf][:, 512 * i:512 * i + 512].rearrange("p (r t) -> p r t", t=4),
-                in0=hs[hf, 0][:, 1024 * a:1024 * a + 1024].rearrange("p (t r) -> p r t", t=4)[:, rows],
-                in1=pos_t[:, 1024 * hf:1024 * hf + 1024].rearrange("p (r t) -> p r t", t=4)[:, rows], op=ADD)
+                in0=hs[hf][:].rearrange("p (t r) -> p r t", t=4)[:, 128 * i:128 * i + 128],
+                in1=pos_t[:, 1024 * hf + 512 * r:1024 * hf + 512 * r + 512].rearrange("p (r t) -> p r t", t=4), op=ADD)
 
         def h_quant(hf, i, n=1):
             w = slice(128 * i, 128 * (i + n))
@@ -216,85 +222,82 @@ def tile_patch_embed_qkv_d4_kernel(tc, x_bytes, x_scale, w_bytes, w_scale, gain,
                 nc.gpsimd.tensor_tensor(out=o, in0=raw[:], in1=b, op=ADD)
             else:
                 nc.vector.tensor_tensor(out=o, in0=ob[n][:], in1=b, op=ADD)
-            if n >= 22:
+            if n in (0, 1, 22, 23):
                 nc.sync.dma_start(out=out[128 * i:128 * i + 128, 512 * c:512 * c + 512], in_=o)
             elif c % 2 == 1:
                 nc.sync.dma_start(out=out[128 * i:128 * i + 128, 512 * c - 512:512 * c + 512], in_=ot[n // 2][:])
 
-        on_vector = [i for i in range(4) if i not in X_ON_SCALAR]
-        on_scalar = list(X_ON_SCALAR)
-        extra = [(g, 1, part) for g in range(G1) for part in range(2)]
+        def x_part(g):
+            x_widen(g, [i for i in range(4) if i in XS[g]])
+            x_widen(g, [i for i in range(4) if i not in XS[g]])
+            for h in range(2):
+                x_turn(g, h)
 
-        def more(k):
-            for j in range(k):
-                if extra:
-                    w_widen(*extra.pop(0))
+        def x_outs(g):
+            for h in range(2):
+                x_out(g, h)
 
-        def w_wide(g):
-            if g < G1:
-                w_widen(g, 0, 0)
-                w_widen(g, 0, 1)
-
-        x_widen(0, on_scalar)
-        x_widen(0, on_vector)
-        w_wide(0)
-        for h in range(2):
-            x_turn(0, h)
-            x_out(0, h)
-        x_widen(1, on_scalar)
-        w_wide(1)
-        for g in range(G1):
-            w_scale_in(g, 0)
-            if g + 1 < G1:
-                x_widen(g + 1, on_vector)
-                x_turn(g + 1, 0)
-                x_turn(g + 1, 1)
-            x_quant(g)
-            w_quant(g, 0)
-            if g + 2 < G1:
-                x_widen(g + 2, on_scalar)
-            w_wide(g + 2)
-            if g + 1 < G1:
-                x_out(g + 1, 0)
-                x_out(g + 1, 1)
-            else:
-                pos_turn()
-            more(MORE[g])
-            mm1(g, 0)
-        w_scale_in(0, 1)
-        for g in range(G1):
-            if g + 1 < G1:
-                w_scale_in(g + 1, 1)
-            w_quant(g, 1)
-            mm1(g, 1)
-            if g < 4:
-                h_gain(0, g, 0)
-                h_gain(0, g, 1)
-            if g == 4:
+        U = 2 * G1
+        x_part(0)
+        w_widen(0)
+        x_outs(0)
+        for u in range(1, AHEAD):
+            if u in V_SCALES:
+                w_widen(u)
+        x_part(1)
+        if 1 not in V_SCALES:
+            w_widen(1)
+        w_scale_in(0)
+        for s in range(U):
+            if s + 2 < G1:
+                x_part(s + 2)
+            if s + 1 < G1:
+                x_outs(s + 1)
+            if s + AHEAD in V_SCALES:
+                w_widen(s + AHEAD)
+            if s == U - 2:
+                w_quant(s)
+            if s + 1 < U:
+                w_scale_in(s + 1)
+            if s < G1:
+                x_quant(s)
+            if s + 2 < U and s + 2 not in V_SCALES:
+                w_widen(s + 2)
+            if s == U - 1:
+                for t in range(4):
+                    h_gain(0, t, 0, 512)
                 h_pos(0, 0)
-                h_pos(0, 1)
-            more(2)
-        h_pos(0, 2)
-        h_quant(0, 0, 2)
-        h_pos(0, 3)
-        h_quant(0, 2, 2)
-        for n in range(4):
-            mm2(n, 0)
-        for a in range(2):
-            for t in range(4):
-                h_gain(1, t, a)
+            if s != U - 2:
+                w_quant(s)
+            mm1(s)
+            if s == 4:
+                pos_turn(0)
+                pos_turn(1)
+        h_pos(0, 1)
+        for t in range(4):
+            h_gain(1, t, 0, 128)
+        for t in range(4):
+            h_gain(1, t, 128, 512)
         h_pos(1, 0)
-        h_pos(1, 1)
+        h_quant(0, 0, 2)
         h_quant(1, 0)
-        h_quant(1, 1)
         for n in range(24):
-            if n >= 4:
-                mm2(n, 0)
-            mm2(n, 1)
             if n == 0:
-                h_pos(1, 2)
-            if n == 1:
-                h_pos(1, 3)
-            if n == 2:
-                h_quant(1, 2, 2)
+                for j in range(4):
+                    mm2(j, 0)
+                    mm2(j, 1)
+            elif n + 3 < 24:
+                mm2(n + 3, 0)
+                mm2(n + 3, 1)
             finish(n)
+            if n == 0:
+                h_pos(1, 1)
+            if n == 1:
+                h_quant(1, 1)
+            if n in (4, 10):
+                h_pos(0, 2 + n // 8)
+            if n in (6, 12):
+                h_pos(1, 2 + n // 8)
+            if n in (7, 13):
+                h_quant(0, 2 + n // 8)
+                h_quant(1, 2 + n // 8)

@@ -18,10 +18,11 @@ COPY = mybir.ActivationFunctionType.Copy
 P = 128
 TOK, K, D, N = 512, 3072, 1024, 3072
 G1 = K // 512
+H_AT = 0
 XS = ((), (), (), (), (), ())
-V_SCALES = tuple(range(12))
-AHEAD = 4
-ON_GPSIMD = (3, 7, 11, 15, 19)
+S_BLOCKS = ((11, 2), (11, 3))
+WIDEN = (1, 2, 1, 2, 1, 1, 1, 1, 0, 0, 0, 0)
+ON_GPSIMD = ()
 FLOPS = 2 * TOK * K * D + 2 * TOK * D * N
 
 
@@ -30,7 +31,7 @@ def tile_patch_embed_qkv_d4_kernel(tc, x_bytes, x_scale, w_bytes, w_scale, gain,
     with ExitStack() as ctx:
         keep = ctx.enter_context(tc.tile_pool(name="keep", bufs=1))
         stage = ctx.enter_context(tc.tile_pool(name="stage", bufs=3))
-        wide = ctx.enter_context(tc.tile_pool(name="wide", bufs=AHEAD + 2))
+        wide = ctx.enter_context(tc.tile_pool(name="wide", bufs=6))
         outs = ctx.enter_context(tc.tile_pool(name="outs", bufs=5))
         psum = ctx.enter_context(tc.psum_pool(name="psum", bufs=1))
         ctx.enter_context(tc.manual_schedule())
@@ -39,24 +40,30 @@ def tile_patch_embed_qkv_d4_kernel(tc, x_bytes, x_scale, w_bytes, w_scale, gain,
             return psum.tile([P, 512], F32, name="bank%d" % b)
 
         xs = keep.tile([P, 4 * 24], F32, name="xs")
-        nc.sync.dma_start(out=xs[:].rearrange("p (i c) -> p i c", i=4), in_=x_scale.rearrange("(i p) c -> p i c", p=P))
+        nc.scalar.dma_start(out=xs[:].rearrange("p (i c) -> p i c", i=4), in_=x_scale.rearrange("(i p) c -> p i c", p=P))
         wall = keep.tile([P, 192], F32, name="wall")
         nc.scalar.dma_start(out=wall[:], in_=w_scale.rearrange("c d -> (c d)").partition_broadcast(P))
 
         x_rows = x_bytes.rearrange("(i p) k -> p i k", p=P)
         xb, wb = {}, {}
 
-        def load_x(g):
-            xb[g] = keep.tile([P, 2048], U8, name="xb%d" % g)
-            nc.sync.dma_start(out=xb[g][:].rearrange("p (i k) -> p i k", i=4), in_=x_rows[:, :, 512 * g:512 * g + 512])
-
-        def load_w(g, hf):
-            wb[g, hf] = keep.tile([P, 2048], U8, name="wb%d_%d" % (g, hf))
+        def load_x(g, part=slice(0, 4)):
+            if g not in xb:
+                xb[g] = keep.tile([P, 2048], U8, name="xb%d" % g)
             nc.sync.dma_start(
-                out=wb[g, hf][:].rearrange("p (t n) -> p t n", t=4),
-                in_=w_bytes[512 * g:512 * g + 512, 512 * hf:512 * hf + 512].rearrange("(p t) n -> p t n", t=4))
+                out=xb[g][:].rearrange("p (i k) -> p i k", i=4)[:, part], in_=x_rows[:, part, 512 * g:512 * g + 512])
 
-        for g in range(G1):
+        def load_w(g, hf, part=slice(0, 4)):
+            if (g, hf) not in wb:
+                wb[g, hf] = keep.tile([P, 2048], U8, name="wb%d_%d" % (g, hf))
+            nc.sync.dma_start(
+                out=wb[g, hf][:].rearrange("p (t n) -> p t n", t=4)[:, part],
+                in_=w_bytes[512 * g:512 * g + 512, 512 * hf:512 * hf + 512].rearrange("(p t) n -> p t n", t=4)[:, part])
+
+        for part in (slice(0, 2), slice(2, 4)):
+            load_x(0, part)
+            load_w(0, 0, part)
+        for g in range(1, G1):
             load_x(g)
             load_w(g, 0)
         pos_sb = keep.tile([P, 2048], BF16, name="pos_sb")
@@ -79,6 +86,8 @@ def tile_patch_embed_qkv_d4_kernel(tc, x_bytes, x_scale, w_bytes, w_scale, gain,
 
         ident = keep.tile([P, P], F32, name="ident")
         make_identity(nc, ident[:])
+        ident_b = keep.tile([P, P], BF16, name="ident_b")
+        nc.gpsimd.tensor_copy(out=ident_b[:], in_=ident[:])
         wsc = keep.tile([P, G1 * 8], F32, name="wsc")
         for q in range(4):
             rows = slice(32 * q, 32 * q + 32)
@@ -129,10 +138,10 @@ def tile_patch_embed_qkv_d4_kernel(tc, x_bytes, x_scale, w_bytes, w_scale, gain,
         def w_widen(u):
             g, hf = u % G1, u // G1
             ww[u] = wide.tile([P, 2048], BF16, name="ww")
-            if u in V_SCALES:
-                nc.scalar.copy(out=ww[u][:], in_=wb[g, hf][:].bitcast(FP8))
-            else:
-                nc.vector.tensor_copy(out=ww[u][:], in_=wb[g, hf][:].bitcast(FP8))
+            parts = 2 if u == 0 else 1
+            for j in range(parts):
+                cols = slice(2048 // parts * j, 2048 // parts * (j + 1))
+                nc.scalar.copy(out=ww[u][:, cols], in_=wb[g, hf][:, cols].bitcast(FP8))
 
         def w_scale_in(u):
             g, hf = u % G1, u // G1
@@ -141,7 +150,7 @@ def tile_patch_embed_qkv_d4_kernel(tc, x_bytes, x_scale, w_bytes, w_scale, gain,
             dst = wint[u][:].rearrange("p (t b m j) -> p b m t j", t=4, b=4, j=4)
             for b in range(4):
                 col = 8 * g + 4 * hf + b
-                if u in V_SCALES:
+                if (u, b) not in S_BLOCKS:
                     nc.vector.tensor_scalar(out=dst[:, b], in0=src[:, b], scalar1=wsc[:, col:col + 1], scalar2=None, op0=MULT)
                 else:
                     nc.scalar.activation(out=dst[:, b], in_=src[:, b], func=COPY, scale=wsc[:, col:col + 1])
@@ -166,33 +175,32 @@ def tile_patch_embed_qkv_d4_kernel(tc, x_bytes, x_scale, w_bytes, w_scale, gain,
         pos_t = keep.tile([P, 2048], BF16, name="pos_t")
 
         def pos_turn(hf):
-            words = pos_sb[:].bitcast(F32)
-            pb = bank(6 + hf)
-            for i in range(2):
-                for u in range(2):
-                    first = 512 * i + 256 * hf
-                    at = 128 * (2 * i + u)
-                    nc.tensor.transpose(pb[:, at:at + 128], words[:, first + u:first + 256:2], ident[:])
-            nc.scalar.copy(
-                out=pos_t[:, 1024 * hf:1024 * hf + 1024].bitcast(F32).rearrange("p (i r u) -> p i r u", i=2, u=2),
-                in_=pb[:].rearrange("p (i u r) -> p i r u", i=2, u=2))
+            pb = psum.tile([P, 1024], BF16, name="bank%d" % (6 + hf))
+            for t in range(4):
+                for i in range(2):
+                    at = 256 * t + 128 * i
+                    first = 1024 * i + 512 * hf + t
+                    nc.tensor.transpose(pb[:, at:at + 128], pos_sb[:, first:first + 509:4], ident_b[:])
+            nc.scalar.copy(out=pos_t[:, 1024 * hf:1024 * hf + 1024], in_=pb[:])
 
         hs, hint = {}, {}
         hq = [keep.tile([P, 512], U32, name="hq%d" % h, align_bytes=64) for h in range(2)]
         hqs = [keep.tile([P, 512], U8, name="hqs%d" % h, align_bytes=64) for h in range(2)]
 
-        def h_gain(hf, t, lo, hi):
+        def h_add(hf, lo, hi):
             if hf not in hs:
-                hs[hf] = keep.tile([P, 2048], F32, name="hs%d" % hf)
+                hs[hf] = keep.tile([P, 2048], BF16, name="hs%d" % hf)
                 hint[hf] = keep.tile([P, 2048], BF16, name="hint%d" % hf, align_bytes=64)
-            nc.scalar.activation(out=hs[hf][:, 512 * t + lo:512 * t + hi], in_=e[hf, t][:, lo:hi], func=COPY, scale=gain_f[:, 4 * hf + t:4 * hf + t + 1])
+            r = lo % 256
+            for t in range(4):
+                nc.vector.scalar_tensor_tensor(
+                    out=hs[hf][:, 512 * t + lo:512 * t + hi], in0=e[hf, t][:, lo:hi], scalar=gain_f[:, 4 * hf + t:4 * hf + t + 1],
+                    in1=pos_t[:, 1024 * hf + 256 * t + r:1024 * hf + 256 * t + r + hi - lo], op0=MULT, op1=ADD)
 
-        def h_pos(hf, i):
-            r = i % 2
-            nc.vector.tensor_tensor(
-                out=hint[hf][:, 512 * i:512 * i + 512].rearrange("p (r t) -> p r t", t=4),
-                in0=hs[hf][:].rearrange("p (t r) -> p r t", t=4)[:, 128 * i:128 * i + 128],
-                in1=pos_t[:, 1024 * hf + 512 * r:1024 * hf + 512 * r + 512].rearrange("p (r t) -> p r t", t=4), op=ADD)
+        def h_weave(hf, i, n=1):
+            nc.scalar.copy(
+                out=hint[hf][:, 512 * i:512 * (i + n)].rearrange("p (r t) -> p r t", t=4),
+                in_=hs[hf][:].rearrange("p (t r) -> p r t", t=4)[:, 128 * i:128 * (i + n)])
 
         def h_quant(hf, i, n=1):
             w = slice(128 * i, 128 * (i + n))
@@ -212,20 +220,23 @@ def tile_patch_embed_qkv_d4_kernel(tc, x_bytes, x_scale, w_bytes, w_scale, gain,
 
         def finish(n):
             i, c = divmod(n, 6)
-            if c % 2 == 0:
-                ot[n // 2] = outs.tile([P, 1024], F32, name="ot")
-            o = ot[n // 2][:, 512 * (c % 2):512 * (c % 2) + 512]
-            b = bias_sb[:, 512 * c:512 * c + 512]
+            rows, cols = slice(128 * i, 128 * i + 128), slice(512 * c, 512 * c + 512)
+            b = bias_sb[:, cols]
             if n in ON_GPSIMD:
                 raw = stage.tile([P, 512], F32, name="raw")
                 nc.scalar.copy(out=raw[:], in_=ob[n][:])
-                nc.gpsimd.tensor_tensor(out=o, in0=raw[:], in1=b, op=ADD)
-            else:
-                nc.vector.tensor_tensor(out=o, in0=ob[n][:], in1=b, op=ADD)
-            if n in (0, 1, 22, 23):
-                nc.sync.dma_start(out=out[128 * i:128 * i + 128, 512 * c:512 * c + 512], in_=o)
+                og = stage.tile([P, 512], F32, name="og")
+                nc.gpsimd.tensor_tensor(out=og[:], in0=raw[:], in1=b, op=ADD)
+                nc.gpsimd.dma_start(out=out[rows, cols], in_=og[:])
+                return
+            if n // 2 not in ot:
+                ot[n // 2] = outs.tile([P, 1024], F32, name="ot")
+            o = ot[n // 2][:, 512 * (c % 2):512 * (c % 2) + 512]
+            nc.vector.tensor_tensor(out=o, in0=ob[n][:], in1=b, op=ADD)
+            if n in (0, 1, 22, 23) or n ^ 1 in ON_GPSIMD:
+                nc.sync.dma_start(out=out[rows, cols], in_=o)
             elif c % 2 == 1:
-                nc.sync.dma_start(out=out[128 * i:128 * i + 128, 512 * c - 512:512 * c + 512], in_=ot[n // 2][:])
+                nc.sync.dma_start(out=out[rows, 512 * c - 512:512 * c + 512], in_=ot[n // 2][:])
 
         def x_part(g):
             x_widen(g, [i for i in range(4) if i in XS[g]])
@@ -238,47 +249,38 @@ def tile_patch_embed_qkv_d4_kernel(tc, x_bytes, x_scale, w_bytes, w_scale, gain,
                 x_out(g, h)
 
         U = 2 * G1
-        x_part(0)
-        w_widen(0)
-        x_outs(0)
-        for u in range(1, AHEAD):
-            if u in V_SCALES:
-                w_widen(u)
-        x_part(1)
-        if 1 not in V_SCALES:
-            w_widen(1)
+        queue = list(range(U))
+        for g in range(2):
+            x_part(g)
+            w_widen(queue.pop(0))
+            x_outs(g)
         w_scale_in(0)
         for s in range(U):
+            for j in range(WIDEN[s]):
+                w_widen(queue.pop(0))
             if s + 2 < G1:
                 x_part(s + 2)
-            if s + 1 < G1:
-                x_outs(s + 1)
-            if s + AHEAD in V_SCALES:
-                w_widen(s + AHEAD)
+                x_outs(s + 2)
+            if s == 4:
+                pos_turn(0)
+                pos_turn(1)
             if s == U - 2:
                 w_quant(s)
             if s + 1 < U:
                 w_scale_in(s + 1)
             if s < G1:
                 x_quant(s)
-            if s + 2 < U and s + 2 not in V_SCALES:
-                w_widen(s + 2)
             if s == U - 1:
-                for t in range(4):
-                    h_gain(0, t, 0, 512)
-                h_pos(0, 0)
+                h_add(0, 0, 256)
+                h_weave(0, 0, 2)
             if s != U - 2:
                 w_quant(s)
             mm1(s)
-            if s == 4:
-                pos_turn(0)
-                pos_turn(1)
-        h_pos(0, 1)
-        for t in range(4):
-            h_gain(1, t, 0, 128)
-        for t in range(4):
-            h_gain(1, t, 128, 512)
-        h_pos(1, 0)
+        h_add(0, 256, 512)
+        h_add(1, 0, 128)
+        h_weave(1, 0)
+        h_add(1, 128, 256)
+        h_weave(1, 1)
         h_quant(0, 0, 2)
         h_quant(1, 0)
         for n in range(24):
@@ -290,14 +292,11 @@ def tile_patch_embed_qkv_d4_kernel(tc, x_bytes, x_scale, w_bytes, w_scale, gain,
                 mm2(n + 3, 0)
                 mm2(n + 3, 1)
             finish(n)
-            if n == 0:
-                h_pos(1, 1)
-            if n == 1:
+            if n == H_AT:
                 h_quant(1, 1)
-            if n in (4, 10):
-                h_pos(0, 2 + n // 8)
-            if n in (6, 12):
-                h_pos(1, 2 + n // 8)
-            if n in (7, 13):
-                h_quant(0, 2 + n // 8)
-                h_quant(1, 2 + n // 8)
+                h_add(1, 256, 512)
+                h_weave(0, 2, 2)
+                h_weave(1, 2, 2)
+            if n == 7:
+                h_quant(0, 2, 2)
+                h_quant(1, 2, 2)

@@ -16,14 +16,19 @@ ADD = mybir.AluOpType.add
 COPY = mybir.ActivationFunctionType.Copy
 
 P = 128
+PASS = 512
 TOK, K, D, N = 512, 3072, 1024, 3072
-G1 = K // 512
-H_AT = 0
-XS = ((), (), (), (), (), ())
-S_BLOCKS = ((11, 2), (11, 3))
-WIDEN = (1, 2, 1, 2, 1, 1, 1, 1, 0, 0, 0, 0)
-ON_GPSIMD = ()
+IMAGE = 256
+PASSES = K // PASS
+UNITS = 2 * PASSES
+TOKEN_TILES = TOK // P
+COLUMN_BLOCKS = N // 512
 FLOPS = 2 * TOK * K * D + 2 * TOK * D * N
+
+VECTOR_WIDENS = (PASSES,)
+SCALAR_SCALES = (UNITS - 1,)
+WIDEN_IN_STEP = (1, 2, 1, 2, 1, 1, 1, 1, 0, 0, 0, 0)
+STORES = ((1, 1, 2, 2), (2, 2, 2), (2, 2, 2), (2, 2, 1, 1))
 
 
 def tile_patch_embed_qkv_d4_kernel(tc, x_bytes, x_scale, w_bytes, w_scale, gain, pos, v_words, v_scales, bias, out):
@@ -36,43 +41,45 @@ def tile_patch_embed_qkv_d4_kernel(tc, x_bytes, x_scale, w_bytes, w_scale, gain,
         psum = ctx.enter_context(tc.psum_pool(name="psum", bufs=1))
         ctx.enter_context(tc.manual_schedule())
 
-        def bank(b):
-            return psum.tile([P, 512], F32, name="bank%d" % b)
+        def bank(b, dtype=F32):
+            return psum.tile([P, 512 if dtype == F32 else 1024], dtype, name="bank%d" % b)
 
-        xs = keep.tile([P, 4 * 24], F32, name="xs")
-        nc.scalar.dma_start(out=xs[:].rearrange("p (i c) -> p i c", i=4), in_=x_scale.rearrange("(i p) c -> p i c", p=P))
-        wall = keep.tile([P, 192], F32, name="wall")
-        nc.scalar.dma_start(out=wall[:], in_=w_scale.rearrange("c d -> (c d)").partition_broadcast(P))
+        ident = keep.tile([P, P], F32, name="ident")
+        make_identity(nc, ident[:])
+        ident_b = keep.tile([P, P], BF16, name="ident_b")
 
-        x_rows = x_bytes.rearrange("(i p) k -> p i k", p=P)
-        xb, wb = {}, {}
+        xs = keep.tile([P, TOKEN_TILES * 24], F32, name="xs")
+        nc.scalar.dma_start(out=xs[:].rearrange("p (i c) -> p i c", i=TOKEN_TILES), in_=x_scale.rearrange("(i p) c -> p i c", p=P))
+        w_scale_all = keep.tile([P, 192], F32, name="w_scale_all")
+        nc.scalar.dma_start(out=w_scale_all[:], in_=w_scale.rearrange("c d -> (c d)").partition_broadcast(P))
 
-        def load_x(g, part=slice(0, 4)):
-            if g not in xb:
-                xb[g] = keep.tile([P, 2048], U8, name="xb%d" % g)
+        xb = [keep.tile([P, 2048], U8, name="xb%d" % g) for g in range(PASSES)]
+        wb = [keep.tile([P, 2048], U8, name="wb%d" % u) for u in range(UNITS)]
+
+        def load_x(g, tiles=slice(0, 4)):
             nc.sync.dma_start(
-                out=xb[g][:].rearrange("p (i k) -> p i k", i=4)[:, part], in_=x_rows[:, part, 512 * g:512 * g + 512])
+                out=xb[g][:].rearrange("p (i k) -> p i k", i=4)[:, tiles],
+                in_=x_bytes.rearrange("(i p) k -> p i k", p=P)[:, tiles, PASS * g:PASS * g + PASS])
 
-        def load_w(g, hf, part=slice(0, 4)):
-            if (g, hf) not in wb:
-                wb[g, hf] = keep.tile([P, 2048], U8, name="wb%d_%d" % (g, hf))
+        def load_w(u, rows=slice(0, 4)):
+            half, g = divmod(u, PASSES)
             nc.sync.dma_start(
-                out=wb[g, hf][:].rearrange("p (t n) -> p t n", t=4)[:, part],
-                in_=w_bytes[512 * g:512 * g + 512, 512 * hf:512 * hf + 512].rearrange("(p t) n -> p t n", t=4)[:, part])
+                out=wb[u][:].rearrange("p (t n) -> p t n", t=4)[:, rows],
+                in_=w_bytes[PASS * g:PASS * g + PASS, 512 * half:512 * half + 512].rearrange("(p t) n -> p t n", t=4)[:, rows])
 
         for part in (slice(0, 2), slice(2, 4)):
             load_x(0, part)
-            load_w(0, 0, part)
-        for g in range(1, G1):
+            load_w(0, part)
+        for g in range(1, PASSES):
             load_x(g)
-            load_w(g, 0)
-        pos_sb = keep.tile([P, 2048], BF16, name="pos_sb")
+            load_w(g)
+        pos_sb = keep.tile([P, 2 * D], BF16, name="pos_sb")
         nc.sync.dma_start(out=pos_sb[:].rearrange("p (i j) -> p i j", i=2), in_=pos.rearrange("(i p) j -> p i j", p=P))
         gain_b = keep.tile([P, 8], BF16, name="gain_b")
         nc.sync.dma_start(out=gain_b[:].rearrange("p (h t) -> p h t", h=2), in_=gain.rearrange("(h p t) -> p h t", h=2, t=4))
-        for g in range(G1):
-            load_w(g, 1)
-        vw = [keep.tile([P, 6144], U8, name="vw%d" % h, align_bytes=64) for h in range(2)]
+        for u in range(PASSES, UNITS):
+            load_w(u)
+        vw = [keep.tile([P, 2 * N], U8, name="vw%d" % h, align_bytes=64) for h in range(2)]
         for h in range(2):
             nc.sync.dma_start(out=vw[h][:].bitcast(I32), in_=v_words[h].bitcast(I32))
         vs = keep.tile([P, 2 * N], U8, name="vs", align_bytes=64)
@@ -84,76 +91,72 @@ def tile_patch_embed_qkv_d4_kernel(tc, x_bytes, x_scale, w_bytes, w_scale, gain,
         bias_sb = keep.tile([P, N], BF16, name="bias_sb")
         nc.sync.dma_start(out=bias_sb[:], in_=bias.partition_broadcast(P))
 
-        ident = keep.tile([P, P], F32, name="ident")
-        make_identity(nc, ident[:])
-        ident_b = keep.tile([P, P], BF16, name="ident_b")
-        nc.gpsimd.tensor_copy(out=ident_b[:], in_=ident[:])
-        wsc = keep.tile([P, G1 * 8], F32, name="wsc")
-        for q in range(4):
-            rows = slice(32 * q, 32 * q + 32)
-            nc.gpsimd.tensor_copy(
-                out=wsc[rows, :].rearrange("p (g d) -> p g d", g=G1),
-                in_=wall[rows, :].rearrange("p (g q d) -> p q g d", q=4, d=8)[:, q])
+        wsc = keep.tile([P, 8 * PASSES], F32, name="wsc")
         gain_f = keep.tile([P, 8], F32, name="gain_f")
-        nc.gpsimd.tensor_copy(out=gain_f[:], in_=gain_b[:])
 
-        xw, xint, xq, xqs = {}, {}, {}, {}
-        xbank = {}
+        def pick_w_scales():
+            for q in range(4):
+                rows = slice(32 * q, 32 * q + 32)
+                nc.scalar.copy(
+                    out=wsc[rows, :].rearrange("p (g d) -> p g d", d=8),
+                    in_=w_scale_all[rows, :].rearrange("p (g q d) -> p q g d", q=4, d=8)[:, q])
 
-        def x_widen(g, tiles):
-            if g not in xw:
-                xw[g] = stage.tile([P, 2048], BF16, name="xw")
-            for i in tiles:
+        xw, xint, xq, xqs, xbank = {}, {}, {}, {}, {}
+
+        def x_widen(g):
+            xw[g] = stage.tile([P, 2048], BF16, name="xw")
+            for i in range(TOKEN_TILES):
                 for c in range(4):
                     cols = slice(512 * i + 128 * c, 512 * i + 128 * c + 128)
                     col = 24 * i + 4 * g + c
-                    if i in XS[g]:
-                        nc.scalar.activation(out=xw[g][:, cols], in_=xb[g][:, cols].bitcast(FP8), func=COPY, scale=xs[:, col:col + 1])
-                    else:
-                        nc.vector.tensor_scalar(out=xw[g][:, cols], in0=xb[g][:, cols].bitcast(FP8), scalar1=xs[:, col:col + 1], scalar2=None, op0=MULT)
+                    nc.vector.tensor_scalar(
+                        out=xw[g][:, cols], in0=xb[g][:, cols].bitcast(FP8), scalar1=xs[:, col:col + 1], scalar2=None, op0=MULT)
 
-        def x_turn(g, h):
+        def x_turn(g):
             words = xw[g][:].bitcast(F32)
-            xbank[g, h] = bank(4 + (2 * g + h) % 4)
-            for i in range(2):
-                for u in range(2):
-                    first = 256 * (2 * h + i)
-                    at = 128 * (2 * i + u)
-                    nc.tensor.transpose(xbank[g, h][:, at:at + 128], words[:, first + u:first + 256:2], ident[:])
+            for b in range(2):
+                xbank[g, b] = bank(4 + (2 * g + b) % 4)
+                for i in range(2):
+                    for u in range(2):
+                        first = 256 * (2 * b + i) + u
+                        at = 128 * (2 * i + u)
+                        nc.tensor.transpose(xbank[g, b][:, at:at + 128], words[:, first:first + 255:2], ident[:])
 
-        def x_out(g, h):
-            if h == 0:
-                xint[g] = stage.tile([P, 2048], BF16, name="xint", align_bytes=64)
-            nc.scalar.copy(
-                out=xint[g][:, 1024 * h:1024 * h + 1024].bitcast(F32).rearrange("p (i r u) -> p i r u", i=2, u=2),
-                in_=xbank[g, h][:].rearrange("p (i u r) -> p i r u", i=2, u=2))
+        def x_out(g):
+            xint[g] = stage.tile([P, 2048], BF16, name="xint", align_bytes=64)
+            for b in range(2):
+                nc.scalar.copy(
+                    out=xint[g][:, 1024 * b:1024 * b + 1024].bitcast(F32).rearrange("p (i r u) -> p i r u", i=2, u=2),
+                    in_=xbank[g, b][:].rearrange("p (i u r) -> p i r u", i=2, u=2))
 
         def x_quant(g):
-            xq[g] = keep.tile([P, 512], U32, name="xq%d" % g, align_bytes=64)
-            xqs[g] = keep.tile([P, 512], U8, name="xqs%d" % g, align_bytes=64)
+            xq[g] = keep.tile([P, TOK], U32, name="xq%d" % g, align_bytes=64)
+            xqs[g] = keep.tile([P, TOK], U8, name="xqs%d" % g, align_bytes=64)
             nc.vector.quantize_mx(out=xq[g][:].bitcast(FP8X4), scales=xqs[g][:], in_=xint[g][:])
 
         ww, wint, wq, wqs = {}, {}, {}, {}
 
         def w_widen(u):
-            g, hf = u % G1, u // G1
             ww[u] = wide.tile([P, 2048], BF16, name="ww")
             parts = 2 if u == 0 else 1
             for j in range(parts):
                 cols = slice(2048 // parts * j, 2048 // parts * (j + 1))
-                nc.scalar.copy(out=ww[u][:, cols], in_=wb[g, hf][:, cols].bitcast(FP8))
+                if u in VECTOR_WIDENS:
+                    nc.vector.tensor_copy(out=ww[u][:, cols], in_=wb[u][:, cols].bitcast(FP8))
+                else:
+                    nc.scalar.copy(out=ww[u][:, cols], in_=wb[u][:, cols].bitcast(FP8))
 
         def w_scale_in(u):
-            g, hf = u % G1, u // G1
+            half, g = divmod(u, PASSES)
             wint[u] = stage.tile([P, 2048], BF16, name="wint", align_bytes=64)
             src = ww[u][:].rearrange("p (j b m t) -> p b m t j", j=4, b=4, t=4)
             dst = wint[u][:].rearrange("p (t b m j) -> p b m t j", t=4, b=4, j=4)
             for b in range(4):
-                col = 8 * g + 4 * hf + b
-                if (u, b) not in S_BLOCKS:
-                    nc.vector.tensor_scalar(out=dst[:, b], in0=src[:, b], scalar1=wsc[:, col:col + 1], scalar2=None, op0=MULT)
-                else:
+                col = 8 * g + 4 * half + b
+                if u in SCALAR_SCALES:
                     nc.scalar.activation(out=dst[:, b], in_=src[:, b], func=COPY, scale=wsc[:, col:col + 1])
+                else:
+                    nc.vector.tensor_scalar(out=dst[:, b], in0=src[:, b], scalar1=wsc[:, col:col + 1], scalar2=None, op0=MULT)
 
         def w_quant(u):
             wq[u] = stage.tile([P, 512], U32, name="wq", align_bytes=64)
@@ -162,141 +165,131 @@ def tile_patch_embed_qkv_d4_kernel(tc, x_bytes, x_scale, w_bytes, w_scale, gain,
 
         e = {}
 
-        def mm1(u):
-            g, hf = u % G1, u // G1
+        def product_1(u):
+            half, g = divmod(u, PASSES)
             for t in range(4):
                 if g == 0:
-                    e[hf, t] = bank(4 * hf + t)
+                    e[half, t] = bank(4 * half + t)
+                cols = slice(128 * t, 128 * t + 128)
                 nc.tensor.matmul_mx(
-                    out=e[hf, t][:],
-                    lhsT=wq[u][:, 128 * t:128 * t + 128].bitcast(FP8X4), lhsT_scale=wqs[u][:, 128 * t:128 * t + 128],
-                    rhs=xq[g][:].bitcast(FP8X4), rhs_scale=xqs[g][:], start=(g == 0), stop=(g == G1 - 1))
+                    out=e[half, t][:],
+                    lhsT=wq[u][:, cols].bitcast(FP8X4), lhsT_scale=wqs[u][:, cols],
+                    rhs=xq[g][:].bitcast(FP8X4), rhs_scale=xqs[g][:], start=(g == 0), stop=(g == PASSES - 1))
 
         pos_t = keep.tile([P, 2048], BF16, name="pos_t")
 
-        def pos_turn(hf):
-            pb = psum.tile([P, 1024], BF16, name="bank%d" % (6 + hf))
+        def pos_turn(half):
+            pb = bank(6 + half, BF16)
             for t in range(4):
                 for i in range(2):
-                    at = 256 * t + 128 * i
-                    first = 1024 * i + 512 * hf + t
+                    first = D * i + 512 * half + t
+                    at = IMAGE * t + 128 * i
                     nc.tensor.transpose(pb[:, at:at + 128], pos_sb[:, first:first + 509:4], ident_b[:])
-            nc.scalar.copy(out=pos_t[:, 1024 * hf:1024 * hf + 1024], in_=pb[:])
+            nc.scalar.copy(out=pos_t[:, 1024 * half:1024 * half + 1024], in_=pb[:])
 
-        hs, hint = {}, {}
-        hq = [keep.tile([P, 512], U32, name="hq%d" % h, align_bytes=64) for h in range(2)]
-        hqs = [keep.tile([P, 512], U8, name="hqs%d" % h, align_bytes=64) for h in range(2)]
+        hs = [keep.tile([P, 4 * TOK], BF16, name="hs%d" % h) for h in range(2)]
+        hint = [keep.tile([P, 4 * TOK], BF16, name="hint%d" % h, align_bytes=64) for h in range(2)]
+        hq = [keep.tile([P, TOK], U32, name="hq%d" % h, align_bytes=64) for h in range(2)]
+        hqs = [keep.tile([P, TOK], U8, name="hqs%d" % h, align_bytes=64) for h in range(2)]
 
-        def h_add(hf, lo, hi):
-            if hf not in hs:
-                hs[hf] = keep.tile([P, 2048], BF16, name="hs%d" % hf)
-                hint[hf] = keep.tile([P, 2048], BF16, name="hint%d" % hf, align_bytes=64)
-            r = lo % 256
-            for t in range(4):
+        def h_add(half, lo, hi, slices=range(4)):
+            r = lo % IMAGE
+            for t in slices:
+                at = 1024 * half + IMAGE * t + r
                 nc.vector.scalar_tensor_tensor(
-                    out=hs[hf][:, 512 * t + lo:512 * t + hi], in0=e[hf, t][:, lo:hi], scalar=gain_f[:, 4 * hf + t:4 * hf + t + 1],
-                    in1=pos_t[:, 1024 * hf + 256 * t + r:1024 * hf + 256 * t + r + hi - lo], op0=MULT, op1=ADD)
+                    out=hs[half][:, TOK * t + lo:TOK * t + hi], in0=e[half, t][:, lo:hi],
+                    scalar=gain_f[:, 4 * half + t:4 * half + t + 1], in1=pos_t[:, at:at + hi - lo], op0=MULT, op1=ADD)
 
-        def h_weave(hf, i, n=1):
+        def h_weave(half, i, n=1):
             nc.scalar.copy(
-                out=hint[hf][:, 512 * i:512 * (i + n)].rearrange("p (r t) -> p r t", t=4),
-                in_=hs[hf][:].rearrange("p (t r) -> p r t", t=4)[:, 128 * i:128 * (i + n)])
+                out=hint[half][:, 512 * i:512 * (i + n)].rearrange("p (r t) -> p r t", t=4),
+                in_=hs[half][:].rearrange("p (t r) -> p r t", t=4)[:, 128 * i:128 * (i + n)])
 
-        def h_quant(hf, i, n=1):
-            w = slice(128 * i, 128 * (i + n))
-            nc.vector.quantize_mx(out=hq[hf][:, w].bitcast(FP8X4), scales=hqs[hf][:, w], in_=hint[hf][:, 512 * i:512 * (i + n)])
+        def h_quant(half, i, n=1):
+            toks = slice(128 * i, 128 * (i + n))
+            nc.vector.quantize_mx(
+                out=hq[half][:, toks].bitcast(FP8X4), scales=hqs[half][:, toks], in_=hint[half][:, 512 * i:512 * (i + n)])
 
         ob, ot = {}, {}
 
-        def mm2(n, h):
-            i, c = divmod(n, 6)
-            if h == 0:
-                ob[n] = bank(n % 8)
-            nc.tensor.matmul_mx(
-                out=ob[n][:],
-                lhsT=hq[h][:, 128 * i:128 * i + 128].bitcast(FP8X4), lhsT_scale=hqs[h][:, 128 * i:128 * i + 128],
-                rhs=vw[h][:, 1024 * c:1024 * c + 1024].bitcast(FP4X4), rhs_scale=vs[:, N * h + 512 * c:N * h + 512 * c + 512],
-                start=(h == 0), stop=(h == 1))
+        def product_2(n):
+            i, c = divmod(n, COLUMN_BLOCKS)
+            ob[n] = bank(n % 8)
+            toks = slice(128 * i, 128 * i + 128)
+            for h in range(2):
+                nc.tensor.matmul_mx(
+                    out=ob[n][:],
+                    lhsT=hq[h][:, toks].bitcast(FP8X4), lhsT_scale=hqs[h][:, toks],
+                    rhs=vw[h][:, 1024 * c:1024 * c + 1024].bitcast(FP4X4), rhs_scale=vs[:, N * h + 512 * c:N * h + 512 * c + 512],
+                    start=(h == 0), stop=(h == 1))
 
         def finish(n):
-            i, c = divmod(n, 6)
-            rows, cols = slice(128 * i, 128 * i + 128), slice(512 * c, 512 * c + 512)
-            b = bias_sb[:, cols]
-            if n in ON_GPSIMD:
-                raw = stage.tile([P, 512], F32, name="raw")
-                nc.scalar.copy(out=raw[:], in_=ob[n][:])
-                og = stage.tile([P, 512], F32, name="og")
-                nc.gpsimd.tensor_tensor(out=og[:], in0=raw[:], in1=b, op=ADD)
-                nc.gpsimd.dma_start(out=out[rows, cols], in_=og[:])
-                return
-            if n // 2 not in ot:
-                ot[n // 2] = outs.tile([P, 1024], F32, name="ot")
-            o = ot[n // 2][:, 512 * (c % 2):512 * (c % 2) + 512]
-            nc.vector.tensor_tensor(out=o, in0=ob[n][:], in1=b, op=ADD)
-            if n in (0, 1, 22, 23) or n ^ 1 in ON_GPSIMD:
-                nc.sync.dma_start(out=out[rows, cols], in_=o)
-            elif c % 2 == 1:
-                nc.sync.dma_start(out=out[rows, 512 * c - 512:512 * c + 512], in_=ot[n // 2][:])
+            i, c = divmod(n, COLUMN_BLOCKS)
+            first, width = 0, STORES[i][0]
+            for k in range(1, len(STORES[i])):
+                if sum(STORES[i][:k]) <= c:
+                    first, width = sum(STORES[i][:k]), STORES[i][k]
+            if c == first:
+                ot[i, first] = outs.tile([P, 1024], F32, name="ot")
+            o = ot[i, first]
+            at = 512 * (c - first)
+            nc.vector.tensor_tensor(out=o[:, at:at + 512], in0=ob[n][:], in1=bias_sb[:, 512 * c:512 * c + 512], op=ADD)
+            if c == first + width - 1:
+                nc.sync.dma_start(out=out[128 * i:128 * i + 128, 512 * first:512 * (c + 1)], in_=o[:, 0:512 * width])
 
-        def x_part(g):
-            x_widen(g, [i for i in range(4) if i in XS[g]])
-            x_widen(g, [i for i in range(4) if i not in XS[g]])
-            for h in range(2):
-                x_turn(g, h)
-
-        def x_outs(g):
-            for h in range(2):
-                x_out(g, h)
-
-        U = 2 * G1
-        queue = list(range(U))
+        nc.scalar.activation(out=ident_b[:], in_=ident[:], func=COPY)
+        to_widen = list(range(UNITS))
         for g in range(2):
-            x_part(g)
-            w_widen(queue.pop(0))
-            x_outs(g)
+            x_widen(g)
+            x_turn(g)
+            w_widen(to_widen.pop(0))
+            if g == 0:
+                pick_w_scales()
+            x_out(g)
         w_scale_in(0)
-        for s in range(U):
-            for j in range(WIDEN[s]):
-                w_widen(queue.pop(0))
-            if s + 2 < G1:
-                x_part(s + 2)
-                x_outs(s + 2)
+        for s in range(UNITS):
+            for j in range(WIDEN_IN_STEP[s]):
+                w_widen(to_widen.pop(0))
+            if s + 2 < PASSES:
+                x_widen(s + 2)
+                x_turn(s + 2)
+                x_out(s + 2)
             if s == 4:
+                nc.scalar.copy(out=gain_f[:], in_=gain_b[:])
                 pos_turn(0)
                 pos_turn(1)
-            if s == U - 2:
+            if s == UNITS - 2:
                 w_quant(s)
-            if s + 1 < U:
+            if s + 1 < UNITS:
                 w_scale_in(s + 1)
-            if s < G1:
+            if s < PASSES:
                 x_quant(s)
-            if s == U - 1:
-                h_add(0, 0, 256)
+            if s == UNITS - 1:
+                h_add(0, 0, IMAGE)
                 h_weave(0, 0, 2)
-            if s != U - 2:
+            if s != UNITS - 2:
                 w_quant(s)
-            mm1(s)
-        h_add(0, 256, 512)
+            product_1(s)
+
+        h_add(0, IMAGE, TOK)
         h_add(1, 0, 128)
         h_weave(1, 0)
-        h_add(1, 128, 256)
+        h_add(1, 128, IMAGE)
         h_weave(1, 1)
         h_quant(0, 0, 2)
         h_quant(1, 0)
-        for n in range(24):
-            if n == 0:
-                for j in range(4):
-                    mm2(j, 0)
-                    mm2(j, 1)
-            elif n + 3 < 24:
-                mm2(n + 3, 0)
-                mm2(n + 3, 1)
+        h_add(1, IMAGE, TOK, range(0, 2))
+        for n in range(4):
+            product_2(n)
+        for n in range(TOKEN_TILES * COLUMN_BLOCKS):
             finish(n)
-            if n == H_AT:
+            if n == 0:
+                h_add(1, IMAGE, TOK, range(2, 4))
                 h_quant(1, 1)
-                h_add(1, 256, 512)
                 h_weave(0, 2, 2)
                 h_weave(1, 2, 2)
             if n == 7:
                 h_quant(0, 2, 2)
                 h_quant(1, 2, 2)
+            if n + 4 < TOKEN_TILES * COLUMN_BLOCKS:
+                product_2(n + 4)

from contextlib import ExitStack

import concourse.mybir as mybir
from concourse.masks import make_identity

F32 = mybir.dt.float32
BF16 = mybir.dt.bfloat16
I32 = mybir.dt.int32
U32 = mybir.dt.uint32
U8 = mybir.dt.uint8
FP8 = mybir.dt.float8_e4m3fn
FP8X4 = mybir.dt.float8_e4m3fn_x4
FP4X4 = mybir.dt.float4_e2m1fn_x4
MULT = mybir.AluOpType.mult
ADD = mybir.AluOpType.add
COPY = mybir.ActivationFunctionType.Copy

P = 128
PASS = 512
TOK, K, D, N = 512, 3072, 1024, 3072
IMAGE = 256
PASSES = K // PASS
UNITS = 2 * PASSES
TOKEN_TILES = TOK // P
COLUMN_BLOCKS = N // 512
FLOPS = 2 * TOK * K * D + 2 * TOK * D * N

VECTOR_WIDENS = (PASSES,)
SCALAR_SCALES = (UNITS - 1,)
WIDEN_IN_STEP = (1, 2, 1, 2, 1, 1, 1, 1, 0, 0, 0, 0)
STORES = ((1, 1, 2, 2), (2, 2, 2), (2, 2, 2), (2, 2, 1, 1))


def tile_patch_embed_qkv_d4_kernel(tc, x_bytes, x_scale, w_bytes, w_scale, gain, pos, v_words, v_scales, bias, out):
    nc = tc.nc
    with ExitStack() as ctx:
        keep = ctx.enter_context(tc.tile_pool(name="keep", bufs=1))
        stage = ctx.enter_context(tc.tile_pool(name="stage", bufs=3))
        wide = ctx.enter_context(tc.tile_pool(name="wide", bufs=6))
        outs = ctx.enter_context(tc.tile_pool(name="outs", bufs=5))
        psum = ctx.enter_context(tc.psum_pool(name="psum", bufs=1))
        ctx.enter_context(tc.manual_schedule())

        def bank(b, dtype=F32):
            return psum.tile([P, 512 if dtype == F32 else 1024], dtype, name="bank%d" % b)

        ident = keep.tile([P, P], F32, name="ident")
        make_identity(nc, ident[:])
        ident_b = keep.tile([P, P], BF16, name="ident_b")

        xs = keep.tile([P, TOKEN_TILES * 24], F32, name="xs")
        nc.scalar.dma_start(out=xs[:].rearrange("p (i c) -> p i c", i=TOKEN_TILES), in_=x_scale.rearrange("(i p) c -> p i c", p=P))
        w_scale_all = keep.tile([P, 192], F32, name="w_scale_all")
        nc.scalar.dma_start(out=w_scale_all[:], in_=w_scale.rearrange("c d -> (c d)").partition_broadcast(P))

        xb = [keep.tile([P, 2048], U8, name="xb%d" % g) for g in range(PASSES)]
        wb = [keep.tile([P, 2048], U8, name="wb%d" % u) for u in range(UNITS)]

        def load_x(g, tiles=slice(0, 4)):
            nc.sync.dma_start(
                out=xb[g][:].rearrange("p (i k) -> p i k", i=4)[:, tiles],
                in_=x_bytes.rearrange("(i p) k -> p i k", p=P)[:, tiles, PASS * g:PASS * g + PASS])

        def load_w(u, rows=slice(0, 4)):
            half, g = divmod(u, PASSES)
            nc.sync.dma_start(
                out=wb[u][:].rearrange("p (t n) -> p t n", t=4)[:, rows],
                in_=w_bytes[PASS * g:PASS * g + PASS, 512 * half:512 * half + 512].rearrange("(p t) n -> p t n", t=4)[:, rows])

        for part in (slice(0, 2), slice(2, 4)):
            load_x(0, part)
            load_w(0, part)
        for g in range(1, PASSES):
            load_x(g)
            load_w(g)
        pos_sb = keep.tile([P, 2 * D], BF16, name="pos_sb")
        nc.sync.dma_start(out=pos_sb[:].rearrange("p (i j) -> p i j", i=2), in_=pos.rearrange("(i p) j -> p i j", p=P))
        gain_b = keep.tile([P, 8], BF16, name="gain_b")
        nc.sync.dma_start(out=gain_b[:].rearrange("p (h t) -> p h t", h=2), in_=gain.rearrange("(h p t) -> p h t", h=2, t=4))
        for u in range(PASSES, UNITS):
            load_w(u)
        vw = [keep.tile([P, 2 * N], U8, name="vw%d" % h, align_bytes=64) for h in range(2)]
        for h in range(2):
            nc.sync.dma_start(out=vw[h][:].bitcast(I32), in_=v_words[h].bitcast(I32))
        vs = keep.tile([P, 2 * N], U8, name="vs", align_bytes=64)
        nc.gpsimd.memset(vs[:].bitcast(I32), 0)
        for q in range(4):
            nc.sync.dma_start(
                out=vs[32 * q:32 * q + 4, :].rearrange("p (h n) -> p h n", h=2).bitcast(I32),
                in_=v_scales[:, 4 * q:4 * q + 4, :].rearrange("h r n -> r h n").bitcast(I32))
        bias_sb = keep.tile([P, N], BF16, name="bias_sb")
        nc.sync.dma_start(out=bias_sb[:], in_=bias.partition_broadcast(P))

        wsc = keep.tile([P, 8 * PASSES], F32, name="wsc")
        gain_f = keep.tile([P, 8], F32, name="gain_f")

        def pick_w_scales():
            for q in range(4):
                rows = slice(32 * q, 32 * q + 32)
                nc.scalar.copy(
                    out=wsc[rows, :].rearrange("p (g d) -> p g d", d=8),
                    in_=w_scale_all[rows, :].rearrange("p (g q d) -> p q g d", q=4, d=8)[:, q])

        xw, xint, xq, xqs, xbank = {}, {}, {}, {}, {}

        def x_widen(g):
            xw[g] = stage.tile([P, 2048], BF16, name="xw")
            for i in range(TOKEN_TILES):
                for c in range(4):
                    cols = slice(512 * i + 128 * c, 512 * i + 128 * c + 128)
                    col = 24 * i + 4 * g + c
                    nc.vector.tensor_scalar(
                        out=xw[g][:, cols], in0=xb[g][:, cols].bitcast(FP8), scalar1=xs[:, col:col + 1], scalar2=None, op0=MULT)

        def x_turn(g):
            words = xw[g][:].bitcast(F32)
            for b in range(2):
                xbank[g, b] = bank(4 + (2 * g + b) % 4)
                for i in range(2):
                    for u in range(2):
                        first = 256 * (2 * b + i) + u
                        at = 128 * (2 * i + u)
                        nc.tensor.transpose(xbank[g, b][:, at:at + 128], words[:, first:first + 255:2], ident[:])

        def x_out(g):
            xint[g] = stage.tile([P, 2048], BF16, name="xint", align_bytes=64)
            for b in range(2):
                nc.scalar.copy(
                    out=xint[g][:, 1024 * b:1024 * b + 1024].bitcast(F32).rearrange("p (i r u) -> p i r u", i=2, u=2),
                    in_=xbank[g, b][:].rearrange("p (i u r) -> p i r u", i=2, u=2))

        def x_quant(g):
            xq[g] = keep.tile([P, TOK], U32, name="xq%d" % g, align_bytes=64)
            xqs[g] = keep.tile([P, TOK], U8, name="xqs%d" % g, align_bytes=64)
            nc.vector.quantize_mx(out=xq[g][:].bitcast(FP8X4), scales=xqs[g][:], in_=xint[g][:])

        ww, wint, wq, wqs = {}, {}, {}, {}

        def w_widen(u):
            ww[u] = wide.tile([P, 2048], BF16, name="ww")
            parts = 2 if u == 0 else 1
            for j in range(parts):
                cols = slice(2048 // parts * j, 2048 // parts * (j + 1))
                if u in VECTOR_WIDENS:
                    nc.vector.tensor_copy(out=ww[u][:, cols], in_=wb[u][:, cols].bitcast(FP8))
                else:
                    nc.scalar.copy(out=ww[u][:, cols], in_=wb[u][:, cols].bitcast(FP8))

        def w_scale_in(u):
            half, g = divmod(u, PASSES)
            wint[u] = stage.tile([P, 2048], BF16, name="wint", align_bytes=64)
            src = ww[u][:].rearrange("p (j b m t) -> p b m t j", j=4, b=4, t=4)
            dst = wint[u][:].rearrange("p (t b m j) -> p b m t j", t=4, b=4, j=4)
            for b in range(4):
                col = 8 * g + 4 * half + b
                if u in SCALAR_SCALES:
                    nc.scalar.activation(out=dst[:, b], in_=src[:, b], func=COPY, scale=wsc[:, col:col + 1])
                else:
                    nc.vector.tensor_scalar(out=dst[:, b], in0=src[:, b], scalar1=wsc[:, col:col + 1], scalar2=None, op0=MULT)

        def w_quant(u):
            wq[u] = stage.tile([P, 512], U32, name="wq", align_bytes=64)
            wqs[u] = stage.tile([P, 512], U8, name="wqs", align_bytes=64)
            nc.vector.quantize_mx(out=wq[u][:].bitcast(FP8X4), scales=wqs[u][:], in_=wint[u][:])

        e = {}

        def product_1(u):
            half, g = divmod(u, PASSES)
            for t in range(4):
                if g == 0:
                    e[half, t] = bank(4 * half + t)
                cols = slice(128 * t, 128 * t + 128)
                nc.tensor.matmul_mx(
                    out=e[half, t][:],
                    lhsT=wq[u][:, cols].bitcast(FP8X4), lhsT_scale=wqs[u][:, cols],
                    rhs=xq[g][:].bitcast(FP8X4), rhs_scale=xqs[g][:], start=(g == 0), stop=(g == PASSES - 1))

        pos_t = keep.tile([P, 2048], BF16, name="pos_t")

        def pos_turn(half):
            pb = bank(6 + half, BF16)
            for t in range(4):
                for i in range(2):
                    first = D * i + 512 * half + t
                    at = IMAGE * t + 128 * i
                    nc.tensor.transpose(pb[:, at:at + 128], pos_sb[:, first:first + 509:4], ident_b[:])
            nc.scalar.copy(out=pos_t[:, 1024 * half:1024 * half + 1024], in_=pb[:])

        hs = [keep.tile([P, 4 * TOK], BF16, name="hs%d" % h) for h in range(2)]
        hint = [keep.tile([P, 4 * TOK], BF16, name="hint%d" % h, align_bytes=64) for h in range(2)]
        hq = [keep.tile([P, TOK], U32, name="hq%d" % h, align_bytes=64) for h in range(2)]
        hqs = [keep.tile([P, TOK], U8, name="hqs%d" % h, align_bytes=64) for h in range(2)]

        def h_add(half, lo, hi, slices=range(4)):
            r = lo % IMAGE
            for t in slices:
                at = 1024 * half + IMAGE * t + r
                nc.vector.scalar_tensor_tensor(
                    out=hs[half][:, TOK * t + lo:TOK * t + hi], in0=e[half, t][:, lo:hi],
                    scalar=gain_f[:, 4 * half + t:4 * half + t + 1], in1=pos_t[:, at:at + hi - lo], op0=MULT, op1=ADD)

        def h_weave(half, i, n=1):
            nc.scalar.copy(
                out=hint[half][:, 512 * i:512 * (i + n)].rearrange("p (r t) -> p r t", t=4),
                in_=hs[half][:].rearrange("p (t r) -> p r t", t=4)[:, 128 * i:128 * (i + n)])

        def h_quant(half, i, n=1):
            toks = slice(128 * i, 128 * (i + n))
            nc.vector.quantize_mx(
                out=hq[half][:, toks].bitcast(FP8X4), scales=hqs[half][:, toks], in_=hint[half][:, 512 * i:512 * (i + n)])

        ob, ot = {}, {}

        def product_2(n):
            i, c = divmod(n, COLUMN_BLOCKS)
            ob[n] = bank(n % 8)
            toks = slice(128 * i, 128 * i + 128)
            for h in range(2):
                nc.tensor.matmul_mx(
                    out=ob[n][:],
                    lhsT=hq[h][:, toks].bitcast(FP8X4), lhsT_scale=hqs[h][:, toks],
                    rhs=vw[h][:, 1024 * c:1024 * c + 1024].bitcast(FP4X4), rhs_scale=vs[:, N * h + 512 * c:N * h + 512 * c + 512],
                    start=(h == 0), stop=(h == 1))

        def finish(n):
            i, c = divmod(n, COLUMN_BLOCKS)
            first, width = 0, STORES[i][0]
            for k in range(1, len(STORES[i])):
                if sum(STORES[i][:k]) <= c:
                    first, width = sum(STORES[i][:k]), STORES[i][k]
            if c == first:
                ot[i, first] = outs.tile([P, 1024], F32, name="ot")
            o = ot[i, first]
            at = 512 * (c - first)
            nc.vector.tensor_tensor(out=o[:, at:at + 512], in0=ob[n][:], in1=bias_sb[:, 512 * c:512 * c + 512], op=ADD)
            if c == first + width - 1:
                nc.sync.dma_start(out=out[128 * i:128 * i + 128, 512 * first:512 * (c + 1)], in_=o[:, 0:512 * width])

        nc.scalar.activation(out=ident_b[:], in_=ident[:], func=COPY)
        to_widen = list(range(UNITS))
        for g in range(2):
            x_widen(g)
            x_turn(g)
            w_widen(to_widen.pop(0))
            if g == 0:
                pick_w_scales()
            x_out(g)
        w_scale_in(0)
        for s in range(UNITS):
            for j in range(WIDEN_IN_STEP[s]):
                w_widen(to_widen.pop(0))
            if s + 2 < PASSES:
                x_widen(s + 2)
                x_turn(s + 2)
                x_out(s + 2)
            if s == 4:
                nc.scalar.copy(out=gain_f[:], in_=gain_b[:])
                pos_turn(0)
                pos_turn(1)
            if s == UNITS - 2:
                w_quant(s)
            if s + 1 < UNITS:
                w_scale_in(s + 1)
            if s < PASSES:
                x_quant(s)
            if s == UNITS - 1:
                h_add(0, 0, IMAGE)
                h_weave(0, 0, 2)
            if s != UNITS - 2:
                w_quant(s)
            product_1(s)

        h_add(0, IMAGE, TOK)
        h_add(1, 0, 128)
        h_weave(1, 0)
        h_add(1, 128, IMAGE)
        h_weave(1, 1)
        h_quant(0, 0, 2)
        h_quant(1, 0)
        h_add(1, IMAGE, TOK, range(0, 2))
        for n in range(4):
            product_2(n)
        for n in range(TOKEN_TILES * COLUMN_BLOCKS):
            finish(n)
            if n == 0:
                h_add(1, IMAGE, TOK, range(2, 4))
                h_quant(1, 1)
                h_weave(0, 2, 2)
                h_weave(1, 2, 2)
            if n == 7:
                h_quant(0, 2, 2)
                h_quant(1, 2, 2)
            if n + 4 < TOKEN_TILES * COLUMN_BLOCKS:
                product_2(n + 4)
